import numpy as np
import ml_dtypes


def mxq(x, axis, fmt="e4m3"):
    dtype, down = {"e4m3": (ml_dtypes.float8_e4m3fn, 7), "e5m2": (ml_dtypes.float8_e5m2, 14)}[fmt]
    v = np.moveaxis(np.asarray(x, np.float32).astype(ml_dtypes.bfloat16).astype(np.float64), axis, -1)
    blocks = v.reshape(v.shape[:-1] + (-1, 32))
    amax = np.abs(blocks).max(-1, keepdims=True)
    byte = np.maximum(np.where(amax > 0, np.frexp(amax)[1] - 1 + 127, 0) - down, 1)
    scale = np.exp2(byte - 127.0)
    codes = (blocks / scale).astype(np.float32).astype(dtype).astype(np.float64)
    return np.moveaxis((codes * scale).reshape(v.shape), -1, axis)


WIDE = False


def mx_kscale(k):
    if not WIDE:
        return np.ones(k)
    levels = np.array([10, -10, 5, -5, 0])
    if k % 512:
        return np.exp2(np.random.permutation(np.resize(levels, k // 32))).repeat(32)
    a = np.empty((k // 512, 16))
    for p in range(k // 512):
        a[p, :8] = np.random.permutation(np.resize(levels, 8))
        for g in range(8):
            far = levels[np.abs(levels - a[p, g]) >= 10]
            a[p, g + 8] = far[np.random.randint(len(far))]
    return np.exp2(a.ravel()).repeat(32)


def f64(x):
    return np.asarray(x).astype(np.float64)


def striped(idx):
    return np.tile(idx.reshape(-1, 16).T, (8, 1)).astype(np.uint16)


def unstriped(offs):
    return offs[:16].T.reshape(-1).astype(np.int64)


def pack_weight(w):
    k, n = w.shape
    w = f64(np.asarray(w, np.float32).astype(ml_dtypes.bfloat16)).reshape(k // 32, 32, n)
    amax = np.abs(w).max(1)
    byte = np.clip(np.where(amax > 0, np.frexp(amax)[1] - 1 + 127 - 7, 1), 1, 254)
    scaled = (w * np.exp2(127.0 - byte)[:, None, :]).reshape(k, n).astype(np.float32)
    words = np.ascontiguousarray(scaled.reshape(k // 512, 128, 4, n).transpose(0, 1, 3, 2)).astype(ml_dtypes.float8_e4m3fn).view(np.uint8)
    return words, np.ascontiguousarray(byte.astype(np.uint8).reshape(k // 512, 16, n))


def unpack_weight(words, scales):
    g, p, n, _ = words.shape
    vals = np.ascontiguousarray(words).view(ml_dtypes.float8_e4m3fn).astype(np.float64) * np.repeat(np.exp2(scales.astype(np.float64) - 127.0), 8, axis=1)[..., None]
    return vals.transpose(0, 1, 3, 2).reshape(g * 512, n)


def relu(v):
    return np.maximum(v, 0.0)

def planes(y):
    n, m = y.shape
    v = y.astype(np.float32).astype(ml_dtypes.bfloat16).astype(np.float64).reshape(n // 32, 32, m)
    top = np.abs(v).max(1)
    byte = np.clip(np.where(top > 0, np.frexp(top)[1] - 1 + 127 - 7, 1), 1, 254)
    codes = (v * np.exp2(127.0 - byte)[:, None, :]).reshape(n, m).astype(np.float32).astype(ml_dtypes.float8_e4m3fn).view(np.uint8)
    words = codes.reshape(n // 512, 128, 4, m).transpose(0, 1, 3, 2)
    return np.ascontiguousarray(words), np.ascontiguousarray(byte.astype(np.uint8).reshape(n // 512, 16, m))


K, T, S, H = 512, 2048, 1024, 512
P = 2 ** 7


def setup_inputs():
    n = np.random.standard_normal
    s = mx_kscale(K)[:, None]
    u = mx_kscale(H)
    packed_xT = pack_weight(n((K, T)) * s)
    packed_w2 = pack_weight(n((H, H)) / np.sqrt(H) / u[:, None])
    return {
        "x_words": packed_xT[0],
        "x_scales": packed_xT[1],
        "w1": (n((K, H)) / np.sqrt(K) / s * u).astype(np.float32),
        "w2_words": packed_w2[0],
        "w2_scales": packed_w2[1],
        "share": np.tile(np.random.uniform(0.1, 0.9, S), (P, 1)).astype(np.float32),
        "offs": striped(np.random.permutation(T)[:S]),
        "par": striped(np.random.permutation(S)[(S * np.random.uniform(0, 1, S) ** 4).astype(np.int64)]),
    }


def reference(x_words, x_scales, w1, w2_words, w2_scales, share, offs, par):
    xq = unpack_weight(x_words, x_scales)[:, unstriped(offs)]
    h = relu(mxq(f64(w1), 0, "e4m3").T @ xq)
    z = h + h[:, unstriped(par)] * f64(share)[:1]
    out_0 = unpack_weight(w2_words, w2_scales).T @ mxq(z, 0, "e4m3")
    return (out_0,) + planes(out_0)

@@ -1,0 +1,213 @@
+from contextlib import ExitStack
+
+import concourse.mybir as mybir
+
+F32 = mybir.dt.float32
+BF16 = mybir.dt.bfloat16
+I32 = mybir.dt.int32
+U32 = mybir.dt.uint32
+U16 = mybir.dt.uint16
+U8 = mybir.dt.uint8
+FP8X4 = mybir.dt.float8_e4m3fn_x4
+ALU = mybir.AluOpType
+ACT = mybir.ActivationFunctionType
+
+P = 128
+PACK = 4
+K = 512
+T = 2048
+S = 1024
+BANK_COLS = 128
+BANKS = S // BANK_COLS
+GROUP_BANKS = (2, 2, 2, 1, 1)
+PIECE_COLS = 256
+LIST_ROWS = 16
+
+FLOPS = 2 * 2 * K * K * S
+
+
+def load_scale_rows(queue, tile, rows):
+    for q in range(4):
+        queue.dma_start(out=tile[32 * q : 32 * q + 4, :].bitcast(I32), in_=rows[4 * q : 4 * q + 4, :].bitcast(I32))
+
+
+def tile_picked_treeup_relu_po_kernel(
+    tc, x_words, x_scales, w1, w2_words, w2_scales, share, offs, par, out_0, out_1, out_2
+):
+    nc = tc.nc
+    with ExitStack() as ctx:
+        keep = ctx.enter_context(tc.tile_pool(name="keep", bufs=1))
+        ring = ctx.enter_context(tc.tile_pool(name="ring", bufs=2))
+        psum = ctx.enter_context(tc.psum_pool(name="psum", bufs=1))
+
+        offs_sb = keep.tile([P, S // LIST_ROWS], U16, name="offs_sb")
+        par_sb = keep.tile([P, S // LIST_ROWS], U16, name="par_sb")
+        x_words_sb = keep.tile([P, T], I32, name="x_words_sb", align_bytes=64)
+        x_scales_sb = keep.tile([P, T], U8, name="x_scales_sb", align_bytes=64)
+        w1_raw = [keep.tile([P, PACK, K // 2], F32, name="w1_raw%d" % u, align_bytes=64) for u in range(2)]
+        w2_words_sb = keep.tile([P, K], I32, name="w2_words_sb", align_bytes=64)
+        w2_scales_sb = keep.tile([P, K], U8, name="w2_scales_sb", align_bytes=64)
+        share_sb = [keep.tile([P, S // 2], F32, name="share_sb%d" % u, align_bytes=64) for u in range(2)]
+
+        nc.vector.memset(x_scales_sb[:].bitcast(I32), 0)
+        nc.vector.memset(w2_scales_sb[:].bitcast(I32), 0)
+
+        w1_rows = w1.rearrange("(p j) c -> p j c", j=PACK)
+        nc.sync.dma_start(offs_sb[:], offs)
+        nc.sync.dma_start(par_sb[:], par)
+        nc.sync.dma_start(out=w1_raw[0][:], in_=w1_rows[:, :, : K // 2])
+        load_scale_rows(nc.sync, x_scales_sb, x_scales[0])
+        nc.sync.dma_start(out=w1_raw[1][:], in_=w1_rows[:, :, K // 2 :])
+        nc.sync.dma_start(out=x_words_sb[:], in_=x_words[0].rearrange("p c r -> p (c r)").bitcast(I32))
+        nc.sync.dma_start(out=w2_words_sb[:], in_=w2_words[0].rearrange("p c r -> p (c r)").bitcast(I32))
+        load_scale_rows(nc.sync, w2_scales_sb, w2_scales[0])
+        for u in range(2):
+            nc.sync.dma_start(out=share_sb[u][:], in_=share[:, u * (S // 2) : (u + 1) * (S // 2)])
+
+        xq_scales = keep.tile([P, S], U8, name="xq_scales", align_bytes=64)
+        xq_words = keep.tile([P, S], U32, name="xq_words", align_bytes=64)
+        nc.vector.tensor_copy(xq_scales[:], x_scales_sb[:].indirect(offs_sb[:]))
+
+        w1_bf = keep.tile([P, PACK, P, PACK], BF16, name="w1_bf", align_bytes=64)
+        for u in range(2):
+            nc.scalar.copy(
+                out=w1_bf[:, :, u * (P // 2) : (u + 1) * (P // 2), :].rearrange("p t m j -> p m j t"),
+                in_=w1_raw[u][:].rearrange("p j (m t) -> p m j t", t=PACK),
+            )
+        w1_codes = keep.tile([P, K], U32, name="w1_codes", align_bytes=64)
+        w1_scales = keep.tile([P, K], U8, name="w1_scales", align_bytes=64)
+        for t in range(PACK):
+            cols = slice(t * P, (t + 1) * P)
+            nc.vector.quantize_mx(
+                out=w1_codes[:, cols].bitcast(FP8X4),
+                scales=w1_scales[:, cols],
+                in_=w1_bf[:, t, :, :].rearrange("p m j -> p (m j)"),
+            )
+
+        for piece in range(S // PIECE_COLS):
+            nc.vector.tensor_copy(
+                xq_words[:, piece * PIECE_COLS : (piece + 1) * PIECE_COLS],
+                x_words_sb[:].bitcast(U32).indirect(
+                    offs_sb[:, piece * PIECE_COLS // LIST_ROWS : (piece + 1) * PIECE_COLS // LIST_ROWS]
+                ),
+            )
+
+        banks = [psum.tile([P, PACK, BANK_COLS], F32, name="bank%d" % c) for c in range(BANKS)]
+        h = [keep.tile([P, S], F32, name="h%d" % t, align_bytes=64) for t in range(PACK)]
+
+        def first_product(t, c):
+            tcols = slice(t * P, (t + 1) * P)
+            cols = slice(c * BANK_COLS, (c + 1) * BANK_COLS)
+            nc.tensor.matmul_mx(
+                out=banks[c][:, t, :],
+                lhsT=w1_codes[:, tcols].bitcast(FP8X4),
+                lhsT_scale=w1_scales[:, tcols],
+                rhs=xq_words[:, cols].bitcast(FP8X4),
+                rhs_scale=xq_scales[:, cols],
+                start=True,
+                stop=True,
+            )
+
+        def relu_out(t, c):
+            nc.scalar.activation(
+                out=h[t][:, c * BANK_COLS : (c + 1) * BANK_COLS], in_=banks[c][:, t, :], func=ACT.Relu
+            )
+
+        early = range(BANKS - PIECE_COLS // BANK_COLS)
+        late = range(BANKS - PIECE_COLS // BANK_COLS, BANKS)
+        for c in early:
+            for t in (0, 1):
+                first_product(t, c)
+            for t in (0, 1):
+                relu_out(t, c)
+        for t in (0, 1):
+            for c in late:
+                first_product(t, c)
+            for c in late:
+                relu_out(t, c)
+        for c in range(BANKS):
+            for t in (2, 3):
+                first_product(t, c)
+        for t in (2, 3):
+            for c in range(BANKS):
+                relu_out(t, c)
+
+        w2_codes = keep.tile([P, K], I32, name="w2_codes", align_bytes=64)
+        w2_planes = keep.tile([P, K], U8, name="w2_planes", align_bytes=64)
+        nc.vector.tensor_copy(
+            out=w2_codes[:].rearrange("p (t m) -> p m t", t=PACK),
+            in_=w2_words_sb[:].rearrange("p (m t) -> p m t", t=PACK),
+        )
+        nc.vector.tensor_copy(
+            out=w2_planes[:].rearrange("p (t m) -> p m t", t=PACK),
+            in_=w2_scales_sb[:].rearrange("p (m t) -> p m t", t=PACK),
+        )
+
+        z_codes = keep.tile([P, S], U32, name="z_codes", align_bytes=64)
+        z_scales = keep.tile([P, S], U8, name="z_scales", align_bytes=64)
+        y_codes = keep.tile([P, S], I32, name="y_codes", align_bytes=64)
+        y_scales = keep.tile([P, S], U8, name="y_scales", align_bytes=64)
+        out_rows = out_0.rearrange("(p t) j -> p t j", t=PACK)
+        out_words = out_1[0].rearrange("p c r -> p (c r)").bitcast(I32)
+
+        first_bank = 0
+        for g, nbanks in enumerate(GROUP_BANKS):
+            width = nbanks * BANK_COLS
+            col0 = first_bank * BANK_COLS
+            gcols = slice(col0, col0 + width)
+            lo = col0 % (S // 2)
+            share_g = share_sb[col0 // (S // 2)][:, lo : lo + width]
+            par_g = par_sb[:, col0 // LIST_ROWS : (col0 + width) // LIST_ROWS]
+            taken = ring.tile([P, PACK, width], F32, name="taken", align_bytes=64)
+            for t in range(PACK):
+                nc.vector.tensor_tensor(taken[:, t, :], h[t][:].indirect(par_g), share_g, ALU.mult)
+            z_bf = ring.tile([P, width, PACK], BF16, name="z_bf", align_bytes=64)
+            for b in range(nbanks):
+                bcols = slice(b * BANK_COLS, (b + 1) * BANK_COLS)
+                nc.vector.scalar_tensor_tensor(
+                    out=z_bf[:, bcols, :],
+                    in0=banks[first_bank + b][:].rearrange("p t j -> p j t"),
+                    scalar=0.0,
+                    in1=taken[:, :, bcols].rearrange("p t j -> p j t"),
+                    op0=ALU.max,
+                    op1=ALU.add,
+                )
+            nc.vector.quantize_mx(
+                out=z_codes[:, gcols].bitcast(FP8X4),
+                scales=z_scales[:, gcols],
+                in_=z_bf[:].rearrange("p j t -> p (j t)"),
+            )
+            y = ring.tile([P, PACK, width], F32, name="y", align_bytes=64)
+            y_bf = ring.tile([P, width, PACK], BF16, name="y_bf", align_bytes=64)
+            for b in range(nbanks):
+                c = first_bank + b
+                cols = slice(c * BANK_COLS, (c + 1) * BANK_COLS)
+                bcols = slice(b * BANK_COLS, (b + 1) * BANK_COLS)
+                for t in range(PACK):
+                    tcols = slice(t * P, (t + 1) * P)
+                    nc.tensor.matmul_mx(
+                        out=banks[c][:, t, :],
+                        lhsT=w2_codes[:, tcols].bitcast(FP8X4),
+                        lhsT_scale=w2_planes[:, tcols],
+                        rhs=z_codes[:, cols].bitcast(FP8X4),
+                        rhs_scale=z_scales[:, cols],
+                        start=True,
+                        stop=True,
+                    )
+                nc.scalar.copy(out=y[:, :, bcols], in_=banks[c][:])
+                if c < BANKS - 1:
+                    nc.scalar.copy(out=y_bf[:, bcols, :], in_=banks[c][:].rearrange("p t j -> p j t"))
+                else:
+                    nc.vector.tensor_copy(out=y_bf[:, bcols, :], in_=y[:, :, bcols].rearrange("p t j -> p j t"))
+            nc.sync.dma_start(out=out_rows[:, :, gcols], in_=y[:])
+            nc.vector.quantize_mx(
+                out=y_codes[:, gcols].bitcast(FP8X4),
+                scales=y_scales[:, gcols],
+                in_=y_bf[:].rearrange("p j t -> p (j t)"),
+            )
+            nc.sync.dma_start(out=out_words[:, gcols], in_=y_codes[:, gcols])
+            first_bank = first_bank + nbanks
+        for q in range(4):
+            nc.sync.dma_start(
+                out=out_2[0][4 * q : 4 * q + 4, :].bitcast(I32), in_=y_scales[32 * q : 32 * q + 4, :].bitcast(I32)
+            )

@@ -135,12 +135,12 @@ def tile_picked_treeup_relu_po_kernel(
         w2_codes = keep.tile([P, K], I32, name="w2_codes", align_bytes=64)
         w2_planes = keep.tile([P, K], U8, name="w2_planes", align_bytes=64)
         nc.vector.tensor_copy(
-            out=w2_codes[:].rearrange("p (t m) -> p m t", t=PACK),
-            in_=w2_words_sb[:].rearrange("p (m t) -> p m t", t=PACK),
+            out=w2_codes[:].rearrange("p (t m) -> p t m", t=PACK),
+            in_=w2_words_sb[:].rearrange("p (m t) -> p t m", t=PACK),
         )
         nc.vector.tensor_copy(
-            out=w2_planes[:].rearrange("p (t m) -> p m t", t=PACK),
-            in_=w2_scales_sb[:].rearrange("p (m t) -> p m t", t=PACK),
+            out=w2_planes[:].rearrange("p (t m) -> p t m", t=PACK),
+            in_=w2_scales_sb[:].rearrange("p (m t) -> p t m", t=PACK),
         )
 
         z_codes = keep.tile([P, S], U32, name="z_codes", align_bytes=64)
@@ -164,13 +164,15 @@ def tile_picked_treeup_relu_po_kernel(
             z_bf = ring.tile([P, width, PACK], BF16, name="z_bf", align_bytes=64)
             for b in range(nbanks):
                 bcols = slice(b * BANK_COLS, (b + 1) * BANK_COLS)
-                nc.vector.scalar_tensor_tensor(
-                    out=z_bf[:, bcols, :],
-                    in0=banks[first_bank + b][:].rearrange("p t j -> p j t"),
-                    scalar=0.0,
-                    in1=taken[:, :, bcols].rearrange("p t j -> p j t"),
-                    op0=ALU.max,
-                    op1=ALU.add,
+                own = keep.tile([P, BANK_COLS // 2, PACK, 2], F32, name="own%d" % (first_bank + b), align_bytes=64)
+                nc.scalar.activation(
+                    out=own[:], in_=banks[first_bank + b][:].rearrange("p t (a i) -> p a t i", i=2), func=ACT.Relu
+                )
+                nc.vector.tensor_tensor(
+                    z_bf[:, bcols, :].rearrange("p (a i) t -> p a t i", i=2),
+                    own[:],
+                    taken[:, :, bcols].rearrange("p t (a i) -> p a t i", i=2),
+                    ALU.add,
                 )
             nc.vector.quantize_mx(
                 out=z_codes[:, gcols].bitcast(FP8X4),
@@ -195,10 +197,13 @@ def tile_picked_treeup_relu_po_kernel(
                         stop=True,
                     )
                 nc.scalar.copy(out=y[:, :, bcols], in_=banks[c][:])
-                if c < BANKS - 1:
+                if c < BANKS - 2:
                     nc.scalar.copy(out=y_bf[:, bcols, :], in_=banks[c][:].rearrange("p t j -> p j t"))
                 else:
-                    nc.vector.tensor_copy(out=y_bf[:, bcols, :], in_=y[:, :, bcols].rearrange("p t j -> p j t"))
+                    nc.vector.tensor_copy(
+                        out=y_bf[:, bcols, :].rearrange("p (a i) t -> p a t i", i=2),
+                        in_=y[:, :, bcols].rearrange("p t (a i) -> p a t i", i=2),
+                    )
             nc.sync.dma_start(out=out_rows[:, :, gcols], in_=y[:])
             nc.vector.quantize_mx(
                 out=y_codes[:, gcols].bitcast(FP8X4),
@@ -208,6 +213,6 @@ def tile_picked_treeup_relu_po_kernel(
             nc.sync.dma_start(out=out_words[:, gcols], in_=y_codes[:, gcols])
             first_bank = first_bank + nbanks
         for q in range(4):
-            nc.sync.dma_start(
+            (nc.sync, nc.scalar)[q % 2].dma_start(
                 out=out_2[0][4 * q : 4 * q + 4, :].bitcast(I32), in_=y_scales[32 * q : 32 * q + 4, :].bitcast(I32)
             )

@@ -19,7 +19,7 @@ T = 2048
 S = 1024
 BANK_COLS = 128
 BANKS = S // BANK_COLS
-GROUP_BANKS = (2, 2, 2, 1, 1)
+GROUP_COLS = (256, 256, 256, 128, 128)
 PIECE_COLS = 256
 LIST_ROWS = 16
 
@@ -150,28 +150,36 @@ def tile_picked_treeup_relu_po_kernel(
         out_rows = out_0.rearrange("(p t) j -> p t j", t=PACK)
         out_words = out_1[0].rearrange("p c r -> p (c r)").bitcast(I32)
 
-        first_bank = 0
-        for g, nbanks in enumerate(GROUP_BANKS):
-            width = nbanks * BANK_COLS
-            col0 = first_bank * BANK_COLS
+        def paired(planes):
+            return planes.rearrange("p t (a i) -> p a t i", i=2)
+
+        def paired_words(rounded):
+            return rounded.rearrange("p (a i) t -> p a t i", i=2)
+
+        own = []
+        for c in range(BANKS):
+            own.append(keep.tile([P, BANK_COLS // 2, PACK, 2], F32, name="own%d" % c, align_bytes=64))
+            nc.scalar.activation(out=own[c][:], in_=paired(banks[c][:]), func=ACT.Relu)
+
+        col0 = 0
+        piece_count = 0
+        for width in GROUP_COLS:
             gcols = slice(col0, col0 + width)
             lo = col0 % (S // 2)
             share_g = share_sb[col0 // (S // 2)][:, lo : lo + width]
             par_g = par_sb[:, col0 // LIST_ROWS : (col0 + width) // LIST_ROWS]
+            piece = min(width, BANK_COLS)
+            starts = range(0, width, piece)
             taken = ring.tile([P, PACK, width], F32, name="taken", align_bytes=64)
             for t in range(PACK):
                 nc.vector.tensor_tensor(taken[:, t, :], h[t][:].indirect(par_g), share_g, ALU.mult)
             z_bf = ring.tile([P, width, PACK], BF16, name="z_bf", align_bytes=64)
-            for b in range(nbanks):
-                bcols = slice(b * BANK_COLS, (b + 1) * BANK_COLS)
-                own = keep.tile([P, BANK_COLS // 2, PACK, 2], F32, name="own%d" % (first_bank + b), align_bytes=64)
-                nc.scalar.activation(
-                    out=own[:], in_=banks[first_bank + b][:].rearrange("p t (a i) -> p a t i", i=2), func=ACT.Relu
-                )
+            for b0 in starts:
+                c, in_bank = divmod(col0 + b0, BANK_COLS)
                 nc.vector.tensor_tensor(
-                    z_bf[:, bcols, :].rearrange("p (a i) t -> p a t i", i=2),
-                    own[:],
-                    taken[:, :, bcols].rearrange("p t (a i) -> p a t i", i=2),
+                    paired_words(z_bf[:, b0 : b0 + piece, :]),
+                    own[c][:, in_bank // 2 : (in_bank + piece) // 2],
+                    paired(taken[:, :, b0 : b0 + piece]),
                     ALU.add,
                 )
             nc.vector.quantize_mx(
@@ -179,16 +187,17 @@ def tile_picked_treeup_relu_po_kernel(
                 scales=z_scales[:, gcols],
                 in_=z_bf[:].rearrange("p j t -> p (j t)"),
             )
-            y = ring.tile([P, PACK, width], F32, name="y", align_bytes=64)
-            y_bf = ring.tile([P, width, PACK], BF16, name="y_bf", align_bytes=64)
-            for b in range(nbanks):
-                c = first_bank + b
-                cols = slice(c * BANK_COLS, (c + 1) * BANK_COLS)
-                bcols = slice(b * BANK_COLS, (b + 1) * BANK_COLS)
+            y = keep.tile([P, PACK, width], F32, name="y%d" % col0, align_bytes=64)
+            y_bf = keep.tile([P, width, PACK], BF16, name="y_bf%d" % col0, align_bytes=64)
+            for b0 in starts:
+                cols = slice(col0 + b0, col0 + b0 + piece)
+                bcols = slice(b0, b0 + piece)
+                acc = banks[piece_count % BANKS][:, :, :piece]
+                piece_count = piece_count + 1
                 for t in range(PACK):
                     tcols = slice(t * P, (t + 1) * P)
                     nc.tensor.matmul_mx(
-                        out=banks[c][:, t, :],
+                        out=acc[:, t, :],
                         lhsT=w2_codes[:, tcols].bitcast(FP8X4),
                         lhsT_scale=w2_planes[:, tcols],
                         rhs=z_codes[:, cols].bitcast(FP8X4),
@@ -196,14 +205,8 @@ def tile_picked_treeup_relu_po_kernel(
                         start=True,
                         stop=True,
                     )
-                nc.scalar.copy(out=y[:, :, bcols], in_=banks[c][:])
-                if c < BANKS - 2:
-                    nc.scalar.copy(out=y_bf[:, bcols, :], in_=banks[c][:].rearrange("p t j -> p j t"))
-                else:
-                    nc.vector.tensor_copy(
-                        out=y_bf[:, bcols, :].rearrange("p (a i) t -> p a t i", i=2),
-                        in_=y[:, :, bcols].rearrange("p t (a i) -> p a t i", i=2),
-                    )
+                nc.scalar.copy(out=y_bf[:, bcols, :], in_=acc.rearrange("p t j -> p j t"))
+                nc.scalar.copy(out=y[:, :, bcols], in_=acc)
             nc.sync.dma_start(out=out_rows[:, :, gcols], in_=y[:])
             nc.vector.quantize_mx(
                 out=y_codes[:, gcols].bitcast(FP8X4),
@@ -211,7 +214,7 @@ def tile_picked_treeup_relu_po_kernel(
                 in_=y_bf[:].rearrange("p j t -> p (j t)"),
             )
             nc.sync.dma_start(out=out_words[:, gcols], in_=y_codes[:, gcols])
-            first_bank = first_bank + nbanks
+            col0 = col0 + width
         for q in range(4):
             (nc.sync, nc.scalar)[q % 2].dma_start(
                 out=out_2[0][4 * q : 4 * q + 4, :].bitcast(I32), in_=y_scales[32 * q : 32 * q + 4, :].bitcast(I32)

@@ -17,18 +17,61 @@ PACK = 4
 K = 512
 T = 2048
 S = 1024
+LIST_ROWS = 16
+QUADRANTS = 4
 BANK_COLS = 128
 BANKS = S // BANK_COLS
-GROUP_COLS = (256, 256, 256, 128, 128)
-PIECE_COLS = 256
-LIST_ROWS = 16
+PICK_COLS = 256
+Z_GROUPS = (2, 2, 1, 1, 1, 1)
+STORE_GROUPS = (2, 2, 2, 1, 1)
+PLANE_GROUPS = (4, 2, 1, 1)
+WORD_GROUPS = (6, 1, 1)
+VECTOR_ROUNDS = 2
 
 FLOPS = 2 * 2 * K * K * S
 
 
-def load_scale_rows(queue, tile, rows):
-    for q in range(4):
-        queue.dma_start(out=tile[32 * q : 32 * q + 4, :].bitcast(I32), in_=rows[4 * q : 4 * q + 4, :].bitcast(I32))
+def runs(counts):
+    return [(sum(counts[:g]), count) for g, count in enumerate(counts)]
+
+
+def run_ends(counts):
+    return {first + count - 1: (first, count) for first, count in runs(counts)}
+
+
+def span(first, count, width):
+    return slice(first * width, (first + count) * width)
+
+
+def load_scale_rows(nc, tile, rows):
+    for q in range(QUADRANTS):
+        nc.sync.dma_start(out=tile[32 * q : 32 * q + 4, :].bitcast(I32), in_=rows[4 * q : 4 * q + 4, :].bitcast(I32))
+
+
+def quantise(nc, codes, scales, cols, rounded):
+    nc.vector.quantize_mx(
+        out=codes[:, cols].bitcast(FP8X4), scales=scales[:, cols], in_=rounded.rearrange("p j t -> p (j t)")
+    )
+
+
+def product(nc, bank, t, weight_codes, weight_scales, codes, scales, cols):
+    nc.tensor.matmul_mx(
+        out=bank[:, t, :],
+        lhsT=weight_codes[:, span(t, 1, P)].bitcast(FP8X4),
+        lhsT_scale=weight_scales[:, span(t, 1, P)],
+        rhs=codes[:, cols].bitcast(FP8X4),
+        rhs_scale=scales[:, cols],
+        start=True,
+        stop=True,
+    )
+
+
+def planes_by_pairs(planes):
+    return planes.rearrange("p t (a i) -> p a t i", i=2)
+
+
+def words_by_pairs(rounded):
+    return rounded.rearrange("p (a i) t -> p a t i", i=2)
 
 
 def tile_picked_treeup_relu_po_kernel(
@@ -56,166 +99,136 @@ def tile_picked_treeup_relu_po_kernel(
         nc.sync.dma_start(offs_sb[:], offs)
         nc.sync.dma_start(par_sb[:], par)
         nc.sync.dma_start(out=w1_raw[0][:], in_=w1_rows[:, :, : K // 2])
-        load_scale_rows(nc.sync, x_scales_sb, x_scales[0])
+        load_scale_rows(nc, x_scales_sb, x_scales[0])
         nc.sync.dma_start(out=w1_raw[1][:], in_=w1_rows[:, :, K // 2 :])
         nc.sync.dma_start(out=x_words_sb[:], in_=x_words[0].rearrange("p c r -> p (c r)").bitcast(I32))
         nc.sync.dma_start(out=w2_words_sb[:], in_=w2_words[0].rearrange("p c r -> p (c r)").bitcast(I32))
-        load_scale_rows(nc.sync, w2_scales_sb, w2_scales[0])
+        load_scale_rows(nc, w2_scales_sb, w2_scales[0])
         for u in range(2):
-            nc.sync.dma_start(out=share_sb[u][:], in_=share[:, u * (S // 2) : (u + 1) * (S // 2)])
+            nc.sync.dma_start(out=share_sb[u][:], in_=share[:, span(u, 1, S // 2)])
 
-        xq_scales = keep.tile([P, S], U8, name="xq_scales", align_bytes=64)
-        xq_words = keep.tile([P, S], U32, name="xq_words", align_bytes=64)
-        nc.vector.tensor_copy(xq_scales[:], x_scales_sb[:].indirect(offs_sb[:]))
+        picked_scales = keep.tile([P, S], U8, name="picked_scales", align_bytes=64)
+        picked_words = keep.tile([P, S], U32, name="picked_words", align_bytes=64)
+        nc.vector.tensor_copy(picked_scales[:], x_scales_sb[:].indirect(offs_sb[:]))
 
         w1_bf = keep.tile([P, PACK, P, PACK], BF16, name="w1_bf", align_bytes=64)
         for u in range(2):
             nc.scalar.copy(
-                out=w1_bf[:, :, u * (P // 2) : (u + 1) * (P // 2), :].rearrange("p t m j -> p m j t"),
+                out=w1_bf[:, :, span(u, 1, P // 2), :].rearrange("p t m j -> p m j t"),
                 in_=w1_raw[u][:].rearrange("p j (m t) -> p m j t", t=PACK),
             )
         w1_codes = keep.tile([P, K], U32, name="w1_codes", align_bytes=64)
         w1_scales = keep.tile([P, K], U8, name="w1_scales", align_bytes=64)
         for t in range(PACK):
-            cols = slice(t * P, (t + 1) * P)
-            nc.vector.quantize_mx(
-                out=w1_codes[:, cols].bitcast(FP8X4),
-                scales=w1_scales[:, cols],
-                in_=w1_bf[:, t, :, :].rearrange("p m j -> p (m j)"),
-            )
+            quantise(nc, w1_codes, w1_scales, span(t, 1, P), w1_bf[:, t, :, :])
 
-        for piece in range(S // PIECE_COLS):
+        for piece in range(S // PICK_COLS):
             nc.vector.tensor_copy(
-                xq_words[:, piece * PIECE_COLS : (piece + 1) * PIECE_COLS],
-                x_words_sb[:].bitcast(U32).indirect(
-                    offs_sb[:, piece * PIECE_COLS // LIST_ROWS : (piece + 1) * PIECE_COLS // LIST_ROWS]
-                ),
+                picked_words[:, span(piece, 1, PICK_COLS)],
+                x_words_sb[:].bitcast(U32).indirect(offs_sb[:, span(piece, 1, PICK_COLS // LIST_ROWS)]),
             )
 
         banks = [psum.tile([P, PACK, BANK_COLS], F32, name="bank%d" % c) for c in range(BANKS)]
         h = [keep.tile([P, S], F32, name="h%d" % t, align_bytes=64) for t in range(PACK)]
 
         def first_product(t, c):
-            tcols = slice(t * P, (t + 1) * P)
-            cols = slice(c * BANK_COLS, (c + 1) * BANK_COLS)
-            nc.tensor.matmul_mx(
-                out=banks[c][:, t, :],
-                lhsT=w1_codes[:, tcols].bitcast(FP8X4),
-                lhsT_scale=w1_scales[:, tcols],
-                rhs=xq_words[:, cols].bitcast(FP8X4),
-                rhs_scale=xq_scales[:, cols],
-                start=True,
-                stop=True,
-            )
+            product(nc, banks[c], t, w1_codes, w1_scales, picked_words, picked_scales, span(c, 1, BANK_COLS))
 
-        def relu_out(t, c):
-            nc.scalar.activation(
-                out=h[t][:, c * BANK_COLS : (c + 1) * BANK_COLS], in_=banks[c][:, t, :], func=ACT.Relu
-            )
+        def relu_plane(t, c):
+            nc.scalar.activation(out=h[t][:, span(c, 1, BANK_COLS)], in_=banks[c][:, t, :], func=ACT.Relu)
 
-        early = range(BANKS - PIECE_COLS // BANK_COLS)
-        late = range(BANKS - PIECE_COLS // BANK_COLS, BANKS)
-        for c in early:
+        early_banks = range(BANKS - PICK_COLS // BANK_COLS)
+        last_banks = range(BANKS - PICK_COLS // BANK_COLS, BANKS)
+        for c in early_banks:
             for t in (0, 1):
                 first_product(t, c)
             for t in (0, 1):
-                relu_out(t, c)
+                relu_plane(t, c)
         for t in (0, 1):
-            for c in late:
+            for c in last_banks:
                 first_product(t, c)
-            for c in late:
-                relu_out(t, c)
+            for c in last_banks:
+                relu_plane(t, c)
         for c in range(BANKS):
             for t in (2, 3):
                 first_product(t, c)
         for t in (2, 3):
             for c in range(BANKS):
-                relu_out(t, c)
+                relu_plane(t, c)
 
-        w2_codes = keep.tile([P, K], I32, name="w2_codes", align_bytes=64)
-        w2_planes = keep.tile([P, K], U8, name="w2_planes", align_bytes=64)
-        nc.vector.tensor_copy(
-            out=w2_codes[:].rearrange("p (t m) -> p t m", t=PACK),
-            in_=w2_words_sb[:].rearrange("p (m t) -> p t m", t=PACK),
-        )
-        nc.vector.tensor_copy(
-            out=w2_planes[:].rearrange("p (t m) -> p t m", t=PACK),
-            in_=w2_scales_sb[:].rearrange("p (m t) -> p t m", t=PACK),
-        )
-
-        z_codes = keep.tile([P, S], U32, name="z_codes", align_bytes=64)
-        z_scales = keep.tile([P, S], U8, name="z_scales", align_bytes=64)
-        y_codes = keep.tile([P, S], I32, name="y_codes", align_bytes=64)
-        y_scales = keep.tile([P, S], U8, name="y_scales", align_bytes=64)
-        out_rows = out_0.rearrange("(p t) j -> p t j", t=PACK)
-        out_words = out_1[0].rearrange("p c r -> p (c r)").bitcast(I32)
-
-        def paired(planes):
-            return planes.rearrange("p t (a i) -> p a t i", i=2)
-
-        def paired_words(rounded):
-            return rounded.rearrange("p (a i) t -> p a t i", i=2)
+        w2_dealt_words = keep.tile([P, K], I32, name="w2_dealt_words", align_bytes=64)
+        w2_dealt_scales = keep.tile([P, K], U8, name="w2_dealt_scales", align_bytes=64)
+        for dealt, loaded in ((w2_dealt_words, w2_words_sb), (w2_dealt_scales, w2_scales_sb)):
+            nc.vector.tensor_copy(
+                out=dealt[:].rearrange("p (t m) -> p t m", t=PACK),
+                in_=loaded[:].rearrange("p (m t) -> p t m", t=PACK),
+            )
 
         own = []
         for c in range(BANKS):
             own.append(keep.tile([P, BANK_COLS // 2, PACK, 2], F32, name="own%d" % c, align_bytes=64))
-            nc.scalar.activation(out=own[c][:], in_=paired(banks[c][:]), func=ACT.Relu)
+            nc.scalar.activation(out=own[c][:], in_=planes_by_pairs(banks[c][:]), func=ACT.Relu)
 
-        col0 = 0
-        piece_count = 0
-        for width in GROUP_COLS:
-            gcols = slice(col0, col0 + width)
-            lo = col0 % (S // 2)
-            share_g = share_sb[col0 // (S // 2)][:, lo : lo + width]
-            par_g = par_sb[:, col0 // LIST_ROWS : (col0 + width) // LIST_ROWS]
-            piece = min(width, BANK_COLS)
-            starts = range(0, width, piece)
-            taken = ring.tile([P, PACK, width], F32, name="taken", align_bytes=64)
+        z_codes = keep.tile([P, S], U32, name="z_codes", align_bytes=64)
+        z_scales = keep.tile([P, S], U8, name="z_scales", align_bytes=64)
+        y_bf = keep.tile([P, S, PACK], BF16, name="y_bf", align_bytes=64)
+        y_codes = keep.tile([P, S], I32, name="y_codes", align_bytes=64)
+        y_scales = keep.tile([P, S], U8, name="y_scales", align_bytes=64)
+        y = {}
+        for first, count in runs(STORE_GROUPS):
+            staged = keep.tile([P, PACK, count * BANK_COLS], F32, name="y%d" % first, align_bytes=64)
+            for b in range(count):
+                y[first + b] = (staged, b)
+        out_rows = out_0.rearrange("(p t) j -> p t j", t=PACK)
+        out_words = out_1[0].rearrange("p c r -> p (c r)").bitcast(I32)
+
+        def make_z(first, count):
+            half, first_in_half = divmod(first, BANKS // 2)
+            taken = ring.tile([P, PACK, count * BANK_COLS], F32, name="taken", align_bytes=64)
             for t in range(PACK):
-                nc.vector.tensor_tensor(taken[:, t, :], h[t][:].indirect(par_g), share_g, ALU.mult)
-            z_bf = ring.tile([P, width, PACK], BF16, name="z_bf", align_bytes=64)
-            for b0 in starts:
-                c, in_bank = divmod(col0 + b0, BANK_COLS)
                 nc.vector.tensor_tensor(
-                    paired_words(z_bf[:, b0 : b0 + piece, :]),
-                    own[c][:, in_bank // 2 : (in_bank + piece) // 2],
-                    paired(taken[:, :, b0 : b0 + piece]),
+                    taken[:, t, :],
+                    h[t][:].indirect(par_sb[:, span(first, count, BANK_COLS // LIST_ROWS)]),
+                    share_sb[half][:, span(first_in_half, count, BANK_COLS)],
+                    ALU.mult,
+                )
+            z_bf = ring.tile([P, count * BANK_COLS, PACK], BF16, name="z_bf", align_bytes=64)
+            for b in range(count):
+                nc.vector.tensor_tensor(
+                    words_by_pairs(z_bf[:, span(b, 1, BANK_COLS), :]),
+                    own[first + b][:],
+                    planes_by_pairs(taken[:, :, span(b, 1, BANK_COLS)]),
                     ALU.add,
                 )
-            nc.vector.quantize_mx(
-                out=z_codes[:, gcols].bitcast(FP8X4),
-                scales=z_scales[:, gcols],
-                in_=z_bf[:].rearrange("p j t -> p (j t)"),
-            )
-            y = keep.tile([P, PACK, width], F32, name="y%d" % col0, align_bytes=64)
-            y_bf = keep.tile([P, width, PACK], BF16, name="y_bf%d" % col0, align_bytes=64)
-            for b0 in starts:
-                cols = slice(col0 + b0, col0 + b0 + piece)
-                bcols = slice(b0, b0 + piece)
-                acc = banks[piece_count % BANKS][:, :, :piece]
-                piece_count = piece_count + 1
-                for t in range(PACK):
-                    tcols = slice(t * P, (t + 1) * P)
-                    nc.tensor.matmul_mx(
-                        out=acc[:, t, :],
-                        lhsT=w2_codes[:, tcols].bitcast(FP8X4),
-                        lhsT_scale=w2_planes[:, tcols],
-                        rhs=z_codes[:, cols].bitcast(FP8X4),
-                        rhs_scale=z_scales[:, cols],
-                        start=True,
-                        stop=True,
-                    )
-                nc.scalar.copy(out=y_bf[:, bcols, :], in_=acc.rearrange("p t j -> p j t"))
-                nc.scalar.copy(out=y[:, :, bcols], in_=acc)
-            nc.sync.dma_start(out=out_rows[:, :, gcols], in_=y[:])
-            nc.vector.quantize_mx(
-                out=y_codes[:, gcols].bitcast(FP8X4),
-                scales=y_scales[:, gcols],
-                in_=y_bf[:].rearrange("p j t -> p (j t)"),
-            )
-            nc.sync.dma_start(out=out_words[:, gcols], in_=y_codes[:, gcols])
-            col0 = col0 + width
-        for q in range(4):
+            quantise(nc, z_codes, z_scales, span(first, count, BANK_COLS), z_bf[:])
+
+        def second_layer(c):
+            cols = span(c, 1, BANK_COLS)
+            for t in range(PACK):
+                product(nc, banks[c], t, w2_dealt_words, w2_dealt_scales, z_codes, z_scales, cols)
+            staged, b = y[c]
+            nc.scalar.copy(out=staged[:, :, span(b, 1, BANK_COLS)], in_=banks[c][:])
+            if c < BANKS - VECTOR_ROUNDS:
+                nc.scalar.copy(out=y_bf[:, cols, :], in_=banks[c][:].rearrange("p t j -> p j t"))
+            else:
+                nc.vector.tensor_copy(
+                    out=words_by_pairs(y_bf[:, cols, :]), in_=planes_by_pairs(staged[:, :, span(b, 1, BANK_COLS)])
+                )
+            if c in run_ends(STORE_GROUPS):
+                nc.sync.dma_start(out=out_rows[:, :, span(*run_ends(STORE_GROUPS)[c], BANK_COLS)], in_=staged[:])
+            if c in run_ends(PLANE_GROUPS):
+                done = span(*run_ends(PLANE_GROUPS)[c], BANK_COLS)
+                quantise(nc, y_codes, y_scales, done, y_bf[:, done, :])
+            if c in run_ends(WORD_GROUPS):
+                done = span(*run_ends(WORD_GROUPS)[c], BANK_COLS)
+                nc.sync.dma_start(out=out_words[:, done], in_=y_codes[:, done])
+
+        for first, count in runs(Z_GROUPS):
+            make_z(first, count)
+            for c in range(first, first + count):
+                second_layer(c)
+
+        for q in range(QUADRANTS):
             (nc.sync, nc.scalar)[q % 2].dma_start(
                 out=out_2[0][4 * q : 4 * q + 4, :].bitcast(I32), in_=y_scales[32 * q : 32 * q + 4, :].bitcast(I32)
             )

@@ -1,6 +1,7 @@
 from contextlib import ExitStack
 
 import concourse.mybir as mybir
+from concourse.masks import make_identity
 
 F32 = mybir.dt.float32
 BF16 = mybir.dt.bfloat16
@@ -21,12 +22,9 @@ LIST_ROWS = 16
 QUADRANTS = 4
 BANK_COLS = 128
 BANKS = S // BANK_COLS
-PICK_COLS = 256
-Z_GROUPS = (2, 2, 1, 1, 1, 1)
-STORE_GROUPS = (2, 2, 2, 1, 1)
-PLANE_GROUPS = (4, 2, 1, 1)
-WORD_GROUPS = (6, 1, 1)
-VECTOR_ROUNDS = 2
+HALF = S // 2
+QUARTER = S // 4
+STORE_GROUPS = (2, 2, 1, 1, 1, 1)
 
 FLOPS = 2 * 2 * K * K * S
 
@@ -80,7 +78,6 @@ def tile_picked_treeup_relu_po_kernel(
     nc = tc.nc
     with ExitStack() as ctx:
         keep = ctx.enter_context(tc.tile_pool(name="keep", bufs=1))
-        ring = ctx.enter_context(tc.tile_pool(name="ring", bufs=2))
         psum = ctx.enter_context(tc.psum_pool(name="psum", bufs=1))
 
         offs_sb = keep.tile([P, S // LIST_ROWS], U16, name="offs_sb")
@@ -90,28 +87,34 @@ def tile_picked_treeup_relu_po_kernel(
         w1_raw = [keep.tile([P, PACK, K // 2], F32, name="w1_raw%d" % u, align_bytes=64) for u in range(2)]
         w2_words_sb = keep.tile([P, K], I32, name="w2_words_sb", align_bytes=64)
         w2_scales_sb = keep.tile([P, K], U8, name="w2_scales_sb", align_bytes=64)
-        share_sb = [keep.tile([P, S // 2], F32, name="share_sb%d" % u, align_bytes=64) for u in range(2)]
+        work = keep.tile([P, (PACK + 1) * HALF], F32, name="work", align_bytes=64)
+        share_low = work[:, span(PACK - 1, 1, HALF)]
+        share_high = keep.tile([P, HALF], F32, name="share_high", align_bytes=64)
+        identity = keep.tile([P, P], F32, name="identity", align_bytes=64)
 
-        nc.vector.memset(x_scales_sb[:].bitcast(I32), 0)
+        nc.vector.memset(x_scales_sb[:, : T // 2].bitcast(I32), 0)
+        nc.gpsimd.memset(x_scales_sb[:, T // 2 :].bitcast(I32), 0)
         nc.vector.memset(w2_scales_sb[:].bitcast(I32), 0)
+        make_identity(nc, identity[:])
 
         w1_rows = w1.rearrange("(p j) c -> p j c", j=PACK)
         nc.sync.dma_start(offs_sb[:], offs)
-        nc.sync.dma_start(par_sb[:], par)
         nc.sync.dma_start(out=w1_raw[0][:], in_=w1_rows[:, :, : K // 2])
         load_scale_rows(nc, x_scales_sb, x_scales[0])
         nc.sync.dma_start(out=w1_raw[1][:], in_=w1_rows[:, :, K // 2 :])
         nc.sync.dma_start(out=x_words_sb[:], in_=x_words[0].rearrange("p c r -> p (c r)").bitcast(I32))
+        nc.sync.dma_start(par_sb[:], par)
         nc.sync.dma_start(out=w2_words_sb[:], in_=w2_words[0].rearrange("p c r -> p (c r)").bitcast(I32))
         load_scale_rows(nc, w2_scales_sb, w2_scales[0])
-        for u in range(2):
-            nc.sync.dma_start(out=share_sb[u][:], in_=share[:, span(u, 1, S // 2)])
+        nc.sync.dma_start(out=share_low, in_=share[:, :HALF])
+        nc.sync.dma_start(out=share_high[:], in_=share[:, HALF:])
 
         picked_scales = keep.tile([P, S], U8, name="picked_scales", align_bytes=64)
         picked_words = keep.tile([P, S], U32, name="picked_words", align_bytes=64)
         nc.vector.tensor_copy(picked_scales[:], x_scales_sb[:].indirect(offs_sb[:]))
 
         w1_bf = keep.tile([P, PACK, P, PACK], BF16, name="w1_bf", align_bytes=64)
+
         for u in range(2):
             nc.scalar.copy(
                 out=w1_bf[:, :, span(u, 1, P // 2), :].rearrange("p t m j -> p m j t"),
@@ -119,42 +122,47 @@ def tile_picked_treeup_relu_po_kernel(
             )
         w1_codes = keep.tile([P, K], U32, name="w1_codes", align_bytes=64)
         w1_scales = keep.tile([P, K], U8, name="w1_scales", align_bytes=64)
-        for t in range(PACK):
-            quantise(nc, w1_codes, w1_scales, span(t, 1, P), w1_bf[:, t, :, :])
-
-        for piece in range(S // PICK_COLS):
+        quantise(nc, w1_codes, w1_scales, slice(0, K), w1_bf[:].rearrange("p t m j -> p (t m) j"))
+        for q in range(4):
             nc.vector.tensor_copy(
-                picked_words[:, span(piece, 1, PICK_COLS)],
-                x_words_sb[:].bitcast(U32).indirect(offs_sb[:, span(piece, 1, PICK_COLS // LIST_ROWS)]),
+                picked_words[:, span(q, 1, QUARTER)],
+                x_words_sb[:].bitcast(U32).indirect(offs_sb[:, span(q, 1, QUARTER // LIST_ROWS)]),
             )
 
-        banks = [psum.tile([P, PACK, BANK_COLS], F32, name="bank%d" % c) for c in range(BANKS)]
+        banks = [psum.tile([P, HALF], F32, name="bank%d" % c) for c in range(BANKS)]
         h = [keep.tile([P, S], F32, name="h%d" % t, align_bytes=64) for t in range(PACK)]
+        own = keep.tile([P, PACK, HALF], F32, name="own", align_bytes=64)
 
-        def first_product(t, c):
-            product(nc, banks[c], t, w1_codes, w1_scales, picked_words, picked_scales, span(c, 1, BANK_COLS))
+        def first_product(t, out, cols):
+            nc.tensor.matmul_mx(
+                out=out,
+                lhsT=w1_codes[:, span(t, 1, P)].bitcast(FP8X4),
+                lhsT_scale=w1_scales[:, span(t, 1, P)],
+                rhs=picked_words[:, cols].bitcast(FP8X4),
+                rhs_scale=picked_scales[:, cols],
+                start=True,
+                stop=True,
+            )
 
-        def relu_plane(t, c):
-            nc.scalar.activation(out=h[t][:, span(c, 1, BANK_COLS)], in_=banks[c][:, t, :], func=ACT.Relu)
+        def first_layer(t, bank, first, count):
+            cols = span(first, count, BANK_COLS)
+            out = banks[bank][:, : count * BANK_COLS]
+            first_product(t, out, cols)
+            nc.scalar.activation(out=h[t][:, cols], in_=out, func=ACT.Relu)
 
-        early_banks = range(BANKS - PICK_COLS // BANK_COLS)
-        last_banks = range(BANKS - PICK_COLS // BANK_COLS, BANKS)
-        for c in early_banks:
-            for t in (0, 1):
-                first_product(t, c)
-            for t in (0, 1):
-                relu_plane(t, c)
-        for t in (0, 1):
-            for c in last_banks:
-                first_product(t, c)
-            for c in last_banks:
-                relu_plane(t, c)
-        for c in range(BANKS):
-            for t in (2, 3):
-                first_product(t, c)
-        for t in (2, 3):
-            for c in range(BANKS):
-                relu_plane(t, c)
+        first_layer(0, 0, 0, 2)
+        first_layer(0, 1, 2, 2)
+        first_layer(0, 2, 4, 2)
+        first_layer(0, 3, 6, 1)
+        first_layer(0, 4, 7, 1)
+        first_layer(1, 5, 0, 4)
+        first_layer(1, 6, 4, 4)
+        first_layer(2, 7, 0, 4)
+        first_layer(2, 0, 4, 4)
+        first_layer(3, 1, 0, 4)
+        first_layer(3, 2, 4, 4)
+        for t in range(PACK):
+            nc.sync.dma_start(out=own[:, t, :], in_=h[t][:, HALF:])
 
         w2_dealt_words = keep.tile([P, K], I32, name="w2_dealt_words", align_bytes=64)
         w2_dealt_scales = keep.tile([P, K], U8, name="w2_dealt_scales", align_bytes=64)
@@ -164,10 +172,13 @@ def tile_picked_treeup_relu_po_kernel(
                 in_=loaded[:].rearrange("p (m t) -> p t m", t=PACK),
             )
 
-        own = []
-        for c in range(BANKS):
-            own.append(keep.tile([P, BANK_COLS // 2, PACK, 2], F32, name="own%d" % c, align_bytes=64))
-            nc.scalar.activation(out=own[c][:], in_=planes_by_pairs(banks[c][:]), func=ACT.Relu)
+        z_turned = [keep.tile([P, K], BF16, name="z_turned%d" % c, align_bytes=64) for c in range(BANKS // 2)]
+        z_stage = [keep.tile([P, 2 * K], BF16, name="z_stage%d" % u, align_bytes=64) for u in range(2)]
+        z_place = {0: (0, 0), 2: (1, 0), 4: (0, 0), 5: (1, 0), 6: (0, 1), 7: (1, 1)}
+
+        def z_bf(first, count):
+            tile, slot = z_place[first]
+            return z_stage[tile][:, span(slot, count, K)]
 
         z_codes = keep.tile([P, S], U32, name="z_codes", align_bytes=64)
         z_scales = keep.tile([P, S], U8, name="z_scales", align_bytes=64)
@@ -182,51 +193,144 @@ def tile_picked_treeup_relu_po_kernel(
         out_rows = out_0.rearrange("(p t) j -> p t j", t=PACK)
         out_words = out_1[0].rearrange("p c r -> p (c r)").bitcast(I32)
 
-        def make_z(first, count):
-            half, first_in_half = divmod(first, BANKS // 2)
-            taken = ring.tile([P, PACK, count * BANK_COLS], F32, name="taken", align_bytes=64)
-            for t in range(PACK):
-                nc.vector.tensor_tensor(
-                    taken[:, t, :],
-                    h[t][:].indirect(par_sb[:, span(first, count, BANK_COLS // LIST_ROWS)]),
-                    share_sb[half][:, span(first_in_half, count, BANK_COLS)],
-                    ALU.mult,
-                )
-            z_bf = ring.tile([P, count * BANK_COLS, PACK], BF16, name="z_bf", align_bytes=64)
-            for b in range(count):
-                nc.vector.tensor_tensor(
-                    words_by_pairs(z_bf[:, span(b, 1, BANK_COLS), :]),
-                    own[first + b][:],
-                    planes_by_pairs(taken[:, :, span(b, 1, BANK_COLS)]),
-                    ALU.add,
-                )
-            quantise(nc, z_codes, z_scales, span(first, count, BANK_COLS), z_bf[:])
+        def gather(out, t, first, count):
+            shares = share_low if first < BANKS // 2 else share_high
+            nc.vector.tensor_tensor(
+                out,
+                h[t][:].indirect(par_sb[:, span(first, count, BANK_COLS // LIST_ROWS)]),
+                shares[:, span(first % (BANKS // 2), count, BANK_COLS)],
+                ALU.mult,
+            )
 
-        def second_layer(c):
+        def planes_in(bank):
+            return banks[bank][:].rearrange("p (t j) -> p t j", t=PACK)
+
+        taken_low = [work[:, span(slot, 1, HALF)] for slot in (0, 1, 2, 4)]
+        sum_bank = {0: 3, 1: 4, 2: 5, 3: 6}
+        word_bank = {0: 7, 2: 0}
+        y_bank = {0: 1, 1: 2, 2: 3, 3: 4, 4: 5, 5: 6, 6: 7}
+
+        def sum_turned(t, c):
             cols = span(c, 1, BANK_COLS)
+            out = planes_in(sum_bank[c])[:, t, :]
+            nc.tensor.matmul(out, h[t][:, cols], identity[:], start=True, stop=False, is_transpose=True)
+            nc.tensor.matmul(out, taken_low[t][:, cols], identity[:], start=False, stop=True, is_transpose=True)
+
+        def round_turned(c):
+            nc.scalar.copy(
+                out=z_turned[c][:].rearrange("j (u m e) -> j u m e", u=2, e=2),
+                in_=banks[sum_bank[c]][:].rearrange("j (u e m) -> j u m e", u=2, e=2),
+            )
+
+        def turn_back(first):
+            bank = banks[word_bank[first]][:].rearrange("p (b u j) -> p b u j", b=2, u=2)
+            for b in range(2):
+                pairs = z_turned[first + b][:].bitcast(F32)
+                for u in range(2):
+                    nc.tensor.transpose(bank[:, b, u, :], pairs[:, span(u, 1, P)], identity[:])
+            nc.scalar.copy(
+                out=z_bf(first, 2).bitcast(F32).rearrange("p (b j u) -> p b j u", b=2, u=2),
+                in_=bank.rearrange("p b u j -> p b j u"),
+            )
+
+        def quantise_z(first, count):
+            cols = span(first, count, BANK_COLS)
+            quantise(nc, z_codes, z_scales, cols, z_bf(first, count).rearrange("p (j t) -> p j t", t=PACK))
+
+        def taken_high(first, count):
+            start = (PACK if first == BANKS - 1 else PACK - 1) * HALF
+            return work[:, start : start + count * HALF].rearrange("p (t j) -> p t j", t=PACK)
+
+        def gather_high(first, count):
             for t in range(PACK):
-                product(nc, banks[c], t, w2_dealt_words, w2_dealt_scales, z_codes, z_scales, cols)
+                gather(taken_high(first, count)[:, t, :], t, first, count)
+
+        def add(c, taken):
+            nc.vector.tensor_tensor(
+                words_by_pairs(z_bf(c, 1).rearrange("p (j t) -> p j t", t=PACK)),
+                planes_by_pairs(own[:, :, span(c - BANKS // 2, 1, BANK_COLS)]),
+                planes_by_pairs(taken),
+                ALU.add,
+            )
+
+        def second_layer(c, scalar_rounds):
+            cols = span(c, 1, BANK_COLS)
+            bank = planes_in(y_bank[c])
+            for t in range(PACK):
+                product(nc, bank, t, w2_dealt_words, w2_dealt_scales, z_codes, z_scales, cols)
             staged, b = y[c]
-            nc.scalar.copy(out=staged[:, :, span(b, 1, BANK_COLS)], in_=banks[c][:])
-            if c < BANKS - VECTOR_ROUNDS:
-                nc.scalar.copy(out=y_bf[:, cols, :], in_=banks[c][:].rearrange("p t j -> p j t"))
-            else:
-                nc.vector.tensor_copy(
-                    out=words_by_pairs(y_bf[:, cols, :]), in_=planes_by_pairs(staged[:, :, span(b, 1, BANK_COLS)])
-                )
+            nc.scalar.copy(out=staged[:, :, span(b, 1, BANK_COLS)], in_=bank)
+            if scalar_rounds:
+                nc.scalar.copy(out=y_bf[:, cols, :], in_=bank.rearrange("p t j -> p j t"))
             if c in run_ends(STORE_GROUPS):
                 nc.sync.dma_start(out=out_rows[:, :, span(*run_ends(STORE_GROUPS)[c], BANK_COLS)], in_=staged[:])
-            if c in run_ends(PLANE_GROUPS):
-                done = span(*run_ends(PLANE_GROUPS)[c], BANK_COLS)
-                quantise(nc, y_codes, y_scales, done, y_bf[:, done, :])
-            if c in run_ends(WORD_GROUPS):
-                done = span(*run_ends(WORD_GROUPS)[c], BANK_COLS)
-                nc.sync.dma_start(out=out_words[:, done], in_=y_codes[:, done])
 
-        for first, count in runs(Z_GROUPS):
-            make_z(first, count)
+        def last_second_layer(c):
+            cols = span(c, 1, BANK_COLS)
+            staged, b = y[c]
+            for pair in range(2):
+                bank = planes_in(pair)
+                planes = span(pair, 1, 2)
+                for t in (2 * pair, 2 * pair + 1):
+                    product(nc, bank, t, w2_dealt_words, w2_dealt_scales, z_codes, z_scales, cols)
+                nc.scalar.copy(out=staged[:, planes, :], in_=bank[:, planes, :])
+                nc.sync.dma_start(out=out_rows[:, planes, cols], in_=staged[:, planes, :])
+
+        def vector_rounds(first, count):
+            nc.vector.tensor_copy(
+                out=words_by_pairs(y_bf[:, span(first, count, BANK_COLS), :]), in_=planes_by_pairs(y[first][0][:])
+            )
+
+        def quantise_y(first, count):
+            done = span(first, count, BANK_COLS)
+            quantise(nc, y_codes, y_scales, done, y_bf[:, done, :])
+
+        def store_words(first, count):
+            done = span(first, count, BANK_COLS)
+            nc.sync.dma_start(out=out_words[:, done], in_=y_codes[:, done])
+
+        def gather_low(t, first, count):
+            gather(taken_low[t][:, span(first, count, BANK_COLS)], t, first, count)
             for c in range(first, first + count):
-                second_layer(c)
+                sum_turned(t, c)
+                if t == PACK - 1:
+                    round_turned(c)
+            if t == PACK - 1 and (first + count) % 2 == 0:
+                turn_back(first + count - 2)
+
+        for t, groups in enumerate(((4,), (4,), (2, 2), (1, 1, 2))):
+            for first, count in runs(groups):
+                gather_low(t, first, count)
+        gather_high(4, 2)
+        quantise_z(0, 2)
+        second_layer(0, True)
+        second_layer(1, True)
+        add(4, taken_high(4, 2)[:, :, :BANK_COLS])
+        quantise_z(2, 2)
+        second_layer(2, True)
+        second_layer(3, True)
+        add(5, taken_high(4, 2)[:, :, BANK_COLS:])
+        quantise_z(4, 1)
+        second_layer(4, True)
+        gather_high(6, 1)
+        quantise_z(5, 1)
+        second_layer(5, False)
+        add(6, taken_high(6, 1))
+        gather_high(7, 1)
+        quantise_z(6, 1)
+        second_layer(6, False)
+        add(7, taken_high(7, 1))
+        quantise_z(7, 1)
+        last_second_layer(7)
+        quantise_y(0, 4)
+        store_words(0, 4)
+        vector_rounds(5, 1)
+        vector_rounds(6, 1)
+        quantise_y(4, 2)
+        quantise_y(6, 1)
+        vector_rounds(7, 1)
+        quantise_y(7, 1)
+        store_words(4, 4)
 
         for q in range(QUADRANTS):
             (nc.sync, nc.scalar)[q % 2].dma_start(

@@ -144,23 +144,25 @@ def tile_picked_treeup_relu_po_kernel(
                 stop=True,
             )
 
-        def first_layer(t, bank, first, count):
-            cols = span(first, count, BANK_COLS)
-            out = banks[bank][:, : count * BANK_COLS]
-            first_product(t, out, cols)
-            nc.scalar.activation(out=h[t][:, cols], in_=out, func=ACT.Relu)
+        def place(bank, slot, count):
+            return banks[bank][:, slot * BANK_COLS : (slot + count) * BANK_COLS]
 
-        first_layer(0, 0, 0, 2)
-        first_layer(0, 1, 2, 2)
-        first_layer(0, 2, 4, 2)
-        first_layer(0, 3, 6, 1)
-        first_layer(0, 4, 7, 1)
-        first_layer(1, 5, 0, 4)
-        first_layer(1, 6, 4, 4)
-        first_layer(2, 7, 0, 4)
-        first_layer(2, 0, 4, 4)
-        first_layer(3, 1, 0, 4)
-        first_layer(3, 2, 4, 4)
+        def relu(t, bank, first, count):
+            nc.scalar.activation(out=h[t][:, span(first, count, BANK_COLS)], in_=place(bank, 0, count), func=ACT.Relu)
+
+        plane0 = ((0, 0, 2), (1, 2, 2), (2, 4, 2), (3, 6, 1), (4, 7, 1))
+        for bank, first, count in plane0:
+            first_product(0, place(bank, 0, count), span(first, count, BANK_COLS))
+            if (first + count) % 2 == 0:
+                q = (first + count) // 2 - 1
+                first_product(1, place(5 + q // 2, 2 * (q % 2), 2), span(q, 1, QUARTER))
+        for bank, first, count in plane0:
+            relu(0, bank, first, count)
+        for t in (1, 2, 3):
+            for u in range(2):
+                if t > 1:
+                    first_product(t, banks[5 + u][:], span(u, 1, HALF))
+                relu(t, 5 + u, 4 * u, 4)
         for t in range(PACK):
             nc.sync.dma_start(out=own[:, t, :], in_=h[t][:, HALF:])
 
@@ -206,15 +208,15 @@ def tile_picked_treeup_relu_po_kernel(
             return banks[bank][:].rearrange("p (t j) -> p t j", t=PACK)
 
         taken_low = [work[:, span(slot, 1, HALF)] for slot in (0, 1, 2, 4)]
-        sum_bank = {0: 3, 1: 4, 2: 5, 3: 6}
-        word_bank = {0: 7, 2: 0}
-        y_bank = {0: 1, 1: 2, 2: 3, 3: 4, 4: 5, 5: 6, 6: 7}
+        sum_bank = {0: 0, 1: 1, 2: 2, 3: 3}
+        word_bank = {0: 7, 2: 4}
+        y_bank = {0: 5, 1: 6, 2: 0, 3: 1, 4: 2, 5: 3, 6: 7}
 
-        def sum_turned(t, c):
-            cols = span(c, 1, BANK_COLS)
+        def turn(t, c, values, start):
             out = planes_in(sum_bank[c])[:, t, :]
-            nc.tensor.matmul(out, h[t][:, cols], identity[:], start=True, stop=False, is_transpose=True)
-            nc.tensor.matmul(out, taken_low[t][:, cols], identity[:], start=False, stop=True, is_transpose=True)
+            nc.tensor.matmul(
+                out, values[:, span(c, 1, BANK_COLS)], identity[:], start=start, stop=not start, is_transpose=True
+            )
 
         def round_turned(c):
             nc.scalar.copy(
@@ -269,7 +271,7 @@ def tile_picked_treeup_relu_po_kernel(
             cols = span(c, 1, BANK_COLS)
             staged, b = y[c]
             for pair in range(2):
-                bank = planes_in(pair)
+                bank = planes_in(4 + pair)
                 planes = span(pair, 1, 2)
                 for t in (2 * pair, 2 * pair + 1):
                     product(nc, bank, t, w2_dealt_words, w2_dealt_scales, z_codes, z_scales, cols)
@@ -290,9 +292,11 @@ def tile_picked_treeup_relu_po_kernel(
             nc.sync.dma_start(out=out_words[:, done], in_=y_codes[:, done])
 
         def gather_low(t, first, count):
+            for c in range(first, first + count):
+                turn(t, c, h[t], True)
             gather(taken_low[t][:, span(first, count, BANK_COLS)], t, first, count)
             for c in range(first, first + count):
-                sum_turned(t, c)
+                turn(t, c, taken_low[t], False)
                 if t == PACK - 1:
                     round_turned(c)
             if t == PACK - 1 and (first + count) % 2 == 0:
@@ -323,14 +327,14 @@ def tile_picked_treeup_relu_po_kernel(
         quantise_z(7, 1)
         last_second_layer(7)
         quantise_y(0, 4)
-        store_words(0, 4)
         vector_rounds(5, 1)
         vector_rounds(6, 1)
         quantise_y(4, 2)
         quantise_y(6, 1)
+        store_words(0, 7)
         vector_rounds(7, 1)
         quantise_y(7, 1)
-        store_words(4, 4)
+        store_words(7, 1)
 
         for q in range(QUADRANTS):
             (nc.sync, nc.scalar)[q % 2].dma_start(

@@ -24,17 +24,13 @@ BANK_COLS = 128
 BANKS = S // BANK_COLS
 HALF = S // 2
 QUARTER = S // 4
-STORE_GROUPS = (2, 2, 1, 1, 1, 1)
+STAGE_GROUPS = (2, 1, 1, 1, 1, 1, 1)
 
 FLOPS = 2 * 2 * K * K * S
 
 
 def runs(counts):
     return [(sum(counts[:g]), count) for g, count in enumerate(counts)]
-
-
-def run_ends(counts):
-    return {first + count - 1: (first, count) for first, count in runs(counts)}
 
 
 def span(first, count, width):
@@ -179,16 +175,19 @@ def tile_picked_treeup_relu_po_kernel(
         z_place = {0: (0, 0), 2: (1, 0), 4: (0, 0), 5: (1, 0), 6: (0, 1), 7: (1, 1)}
 
         def z_bf(first, count):
+            if first == BANKS - 1:
+                return y_bf[:, :K]
             tile, slot = z_place[first]
             return z_stage[tile][:, span(slot, count, K)]
 
         z_codes = keep.tile([P, S], U32, name="z_codes", align_bytes=64)
         z_scales = keep.tile([P, S], U8, name="z_scales", align_bytes=64)
-        y_bf = keep.tile([P, S, PACK], BF16, name="y_bf", align_bytes=64)
+        y_bf = keep.tile([P, S * PACK], BF16, name="y_bf", align_bytes=64)
+        y_words = y_bf[:].rearrange("p (j t) -> p j t", t=PACK)
         y_codes = keep.tile([P, S], I32, name="y_codes", align_bytes=64)
         y_scales = keep.tile([P, S], U8, name="y_scales", align_bytes=64)
         y = {}
-        for first, count in runs(STORE_GROUPS):
+        for first, count in runs(STAGE_GROUPS):
             staged = keep.tile([P, PACK, count * BANK_COLS], F32, name="y%d" % first, align_bytes=64)
             for b in range(count):
                 y[first + b] = (staged, b)
@@ -262,30 +261,37 @@ def tile_picked_treeup_relu_po_kernel(
                 product(nc, bank, t, w2_dealt_words, w2_dealt_scales, z_codes, z_scales, cols)
             staged, b = y[c]
             nc.scalar.copy(out=staged[:, :, span(b, 1, BANK_COLS)], in_=bank)
+            nc.sync.dma_start(out=out_rows[:, :, cols], in_=staged[:, :, span(b, 1, BANK_COLS)])
             if scalar_rounds:
-                nc.scalar.copy(out=y_bf[:, cols, :], in_=bank.rearrange("p t j -> p j t"))
-            if c in run_ends(STORE_GROUPS):
-                nc.sync.dma_start(out=out_rows[:, :, span(*run_ends(STORE_GROUPS)[c], BANK_COLS)], in_=staged[:])
+                nc.scalar.copy(out=y_words[:, cols, :], in_=bank.rearrange("p t j -> p j t"))
 
-        def last_second_layer(c):
-            cols = span(c, 1, BANK_COLS)
-            staged, b = y[c]
+        def second_layer_by_pairs(first, count, pair_banks):
+            cols = span(first, count, BANK_COLS)
+            staged = y[first][0]
             for pair in range(2):
-                bank = planes_in(4 + pair)
+                bank = banks[pair_banks[pair]][:, : count * 2 * BANK_COLS].rearrange("p (t j) -> p t j", t=2)
+                for t in range(2):
+                    nc.tensor.matmul_mx(
+                        out=bank[:, t, :],
+                        lhsT=w2_dealt_words[:, span(2 * pair + t, 1, P)].bitcast(FP8X4),
+                        lhsT_scale=w2_dealt_scales[:, span(2 * pair + t, 1, P)],
+                        rhs=z_codes[:, cols].bitcast(FP8X4),
+                        rhs_scale=z_scales[:, cols],
+                        start=True,
+                        stop=True,
+                    )
                 planes = span(pair, 1, 2)
-                for t in (2 * pair, 2 * pair + 1):
-                    product(nc, bank, t, w2_dealt_words, w2_dealt_scales, z_codes, z_scales, cols)
-                nc.scalar.copy(out=staged[:, planes, :], in_=bank[:, planes, :])
+                nc.scalar.copy(out=staged[:, planes, :], in_=bank)
                 nc.sync.dma_start(out=out_rows[:, planes, cols], in_=staged[:, planes, :])
 
         def vector_rounds(first, count):
             nc.vector.tensor_copy(
-                out=words_by_pairs(y_bf[:, span(first, count, BANK_COLS), :]), in_=planes_by_pairs(y[first][0][:])
+                out=words_by_pairs(y_words[:, span(first, count, BANK_COLS), :]), in_=planes_by_pairs(y[first][0][:])
             )
 
         def quantise_y(first, count):
             done = span(first, count, BANK_COLS)
-            quantise(nc, y_codes, y_scales, done, y_bf[:, done, :])
+            quantise(nc, y_codes, y_scales, done, y_words[:, done, :])
 
         def store_words(first, count):
             done = span(first, count, BANK_COLS)
@@ -307,8 +313,7 @@ def tile_picked_treeup_relu_po_kernel(
                 gather_low(t, first, count)
         gather_high(4, 2)
         quantise_z(0, 2)
-        second_layer(0, True)
-        second_layer(1, True)
+        second_layer_by_pairs(0, 2, (5, 6))
         add(4, taken_high(4, 2)[:, :, :BANK_COLS])
         quantise_z(2, 2)
         second_layer(2, True)
@@ -318,17 +323,16 @@ def tile_picked_treeup_relu_po_kernel(
         second_layer(4, True)
         gather_high(6, 1)
         quantise_z(5, 1)
-        second_layer(5, False)
+        second_layer(5, True)
         add(6, taken_high(6, 1))
         gather_high(7, 1)
         quantise_z(6, 1)
-        second_layer(6, False)
+        second_layer(6, True)
         add(7, taken_high(7, 1))
         quantise_z(7, 1)
-        last_second_layer(7)
+        second_layer_by_pairs(7, 1, (4, 5))
+        vector_rounds(0, 2)
         quantise_y(0, 4)
-        vector_rounds(5, 1)
-        vector_rounds(6, 1)
         quantise_y(4, 2)
         quantise_y(6, 1)
         store_words(0, 7)

@@ -209,7 +209,7 @@ def tile_picked_treeup_relu_po_kernel(
         taken_low = [work[:, span(slot, 1, HALF)] for slot in (0, 1, 2, 4)]
         sum_bank = {0: 0, 1: 1, 2: 2, 3: 3}
         word_bank = {0: 7, 2: 4}
-        y_bank = {0: 5, 1: 6, 2: 0, 3: 1, 4: 2, 5: 3, 6: 7}
+        y_bank = {0: 5, 1: 6, 2: 0, 3: 1, 4: 2, 5: 3, 6: 7, 7: 4}
 
         def turn(t, c, values, start):
             out = planes_in(sum_bank[c])[:, t, :]
@@ -284,14 +284,16 @@ def tile_picked_treeup_relu_po_kernel(
                 nc.scalar.copy(out=staged[:, planes, :], in_=bank)
                 nc.sync.dma_start(out=out_rows[:, planes, cols], in_=staged[:, planes, :])
 
+        def rounded_y(first, count):
+            start = (2 if first == 0 else first) * BANK_COLS
+            return y_words[:, start : start + count * BANK_COLS, :]
+
         def vector_rounds(first, count):
-            nc.vector.tensor_copy(
-                out=words_by_pairs(y_words[:, span(first, count, BANK_COLS), :]), in_=planes_by_pairs(y[first][0][:])
-            )
+            nc.vector.tensor_copy(out=words_by_pairs(rounded_y(first, count)), in_=planes_by_pairs(y[first][0][:]))
 
         def quantise_y(first, count):
-            done = span(first, count, BANK_COLS)
-            quantise(nc, y_codes, y_scales, done, y_words[:, done, :])
+            done = slice(first * BANK_COLS, (first + count) * BANK_COLS)
+            quantise(nc, y_codes, y_scales, done, rounded_y(first, count))
 
         def store_words(first, count):
             done = span(first, count, BANK_COLS)
@@ -330,15 +332,15 @@ def tile_picked_treeup_relu_po_kernel(
         second_layer(6, True)
         add(7, taken_high(7, 1))
         quantise_z(7, 1)
-        second_layer_by_pairs(7, 1, (4, 5))
+        second_layer(7, True)
+        quantise_y(2, 4)
+        store_words(2, 4)
         vector_rounds(0, 2)
-        quantise_y(0, 4)
-        quantise_y(4, 2)
         quantise_y(6, 1)
-        store_words(0, 7)
-        vector_rounds(7, 1)
+        quantise_y(0, 2)
+        store_words(0, 2)
         quantise_y(7, 1)
-        store_words(7, 1)
+        store_words(6, 2)
 
         for q in range(QUADRANTS):
             (nc.sync, nc.scalar)[q % 2].dma_start(

@@ -74,51 +74,62 @@ def tile_picked_treeup_relu_po_kernel(
     nc = tc.nc
     with ExitStack() as ctx:
         keep = ctx.enter_context(tc.tile_pool(name="keep", bufs=1))
+        reused = ctx.enter_context(tc.tile_pool(name="reused", bufs=1))
         psum = ctx.enter_context(tc.psum_pool(name="psum", bufs=1))
 
         offs_sb = keep.tile([P, S // LIST_ROWS], U16, name="offs_sb")
         par_sb = keep.tile([P, S // LIST_ROWS], U16, name="par_sb")
         x_words_sb = keep.tile([P, T], I32, name="x_words_sb", align_bytes=64)
-        x_scales_sb = keep.tile([P, T], U8, name="x_scales_sb", align_bytes=64)
-        w1_raw = [keep.tile([P, PACK, K // 2], F32, name="w1_raw%d" % u, align_bytes=64) for u in range(2)]
-        w2_words_sb = keep.tile([P, K], I32, name="w2_words_sb", align_bytes=64)
-        w2_scales_sb = keep.tile([P, K], U8, name="w2_scales_sb", align_bytes=64)
-        work = keep.tile([P, (PACK + 1) * HALF], F32, name="work", align_bytes=64)
+        x_scales_sb = reused.tile([P, T], U8, name="x_scales_sb", align_bytes=64, offset=14336)
+        w1_raw = [
+            reused.tile([P, PACK, K // 2], F32, name="w1_raw%d" % u, align_bytes=64, offset=4096 * u) for u in range(2)
+        ]
+        w2_words_sb = reused.tile([P, K], I32, name="w2_words_sb", align_bytes=64, offset=0)
+        w2_scales_sb = reused.tile([P, K], U8, name="w2_scales_sb", align_bytes=64, offset=14336)
+        work = reused.tile([P, (PACK + 1) * HALF], F32, name="work", align_bytes=64, offset=4096)
         share_low = work[:, span(PACK - 1, 1, HALF)]
-        share_high = keep.tile([P, HALF], F32, name="share_high", align_bytes=64)
+        share_high = reused.tile([P, HALF], F32, name="share_high", align_bytes=64, offset=2048)
         identity = keep.tile([P, P], F32, name="identity", align_bytes=64)
 
-        nc.vector.memset(x_scales_sb[:, : T // 2].bitcast(I32), 0)
-        nc.gpsimd.memset(x_scales_sb[:, T // 2 :].bitcast(I32), 0)
-        nc.vector.memset(w2_scales_sb[:].bitcast(I32), 0)
+        nc.gpsimd.memset(x_scales_sb[0:16, :].bitcast(I32), 0)
+        nc.vector.memset(x_scales_sb[32:64, :].bitcast(I32), 0)
+        nc.vector.memset(x_scales_sb[64:P, :].bitcast(I32), 0)
+        picked_scales = keep.tile([P, S], U8, name="picked_scales", align_bytes=64)
+        nc.vector.memset(picked_scales[:].bitcast(I32), 0)
         make_identity(nc, identity[:])
 
         w1_rows = w1.rearrange("(p j) c -> p j c", j=PACK)
         nc.sync.dma_start(offs_sb[:], offs)
+        nc.sync.dma_start(out=x_scales_sb[16:32, :].bitcast(I32), in_=x_scales[0].bitcast(I32))
         nc.sync.dma_start(out=w1_raw[0][:], in_=w1_rows[:, :, : K // 2])
-        load_scale_rows(nc, x_scales_sb, x_scales[0])
         nc.sync.dma_start(out=w1_raw[1][:], in_=w1_rows[:, :, K // 2 :])
         nc.sync.dma_start(out=x_words_sb[:], in_=x_words[0].rearrange("p c r -> p (c r)").bitcast(I32))
+        picked_rows = keep.tile([P, S], U8, name="picked_rows", align_bytes=64)
+        nc.vector.tensor_copy(picked_rows[:], x_scales_sb[:].indirect(offs_sb[:]))
+        for q in range(QUADRANTS):
+            nc.sync.dma_start(
+                out=picked_scales[32 * q : 32 * q + 4, :].bitcast(I32),
+                in_=picked_rows[16 + 4 * q : 20 + 4 * q, :].bitcast(I32),
+            )
         nc.sync.dma_start(par_sb[:], par)
-        nc.sync.dma_start(out=w2_words_sb[:], in_=w2_words[0].rearrange("p c r -> p (c r)").bitcast(I32))
-        load_scale_rows(nc, w2_scales_sb, w2_scales[0])
-        nc.sync.dma_start(out=share_low, in_=share[:, :HALF])
-        nc.sync.dma_start(out=share_high[:], in_=share[:, HALF:])
 
-        picked_scales = keep.tile([P, S], U8, name="picked_scales", align_bytes=64)
-        picked_words = keep.tile([P, S], U32, name="picked_words", align_bytes=64)
-        nc.vector.tensor_copy(picked_scales[:], x_scales_sb[:].indirect(offs_sb[:]))
 
-        w1_bf = keep.tile([P, PACK, P, PACK], BF16, name="w1_bf", align_bytes=64)
+        w1_bf = reused.tile([P, PACK, P, PACK], BF16, name="w1_bf", align_bytes=64, offset=16384)
 
         for u in range(2):
             nc.scalar.copy(
                 out=w1_bf[:, :, span(u, 1, P // 2), :].rearrange("p t m j -> p m j t"),
                 in_=w1_raw[u][:].rearrange("p j (m t) -> p m j t", t=PACK),
             )
+        nc.sync.dma_start(out=w2_words_sb[:], in_=w2_words[0].rearrange("p c r -> p (c r)").bitcast(I32))
+        nc.vector.memset(w2_scales_sb[:].bitcast(I32), 0)
+        load_scale_rows(nc, w2_scales_sb, w2_scales[0])
+        nc.sync.dma_start(out=share_low, in_=share[:, :HALF])
+        nc.sync.dma_start(out=share_high[:], in_=share[:, HALF:])
         w1_codes = keep.tile([P, K], U32, name="w1_codes", align_bytes=64)
         w1_scales = keep.tile([P, K], U8, name="w1_scales", align_bytes=64)
         quantise(nc, w1_codes, w1_scales, slice(0, K), w1_bf[:].rearrange("p t m j -> p (t m) j"))
+        picked_words = reused.tile([P, S], U32, name="picked_words", align_bytes=64, offset=16384)
         for q in range(4):
             nc.vector.tensor_copy(
                 picked_words[:, span(q, 1, QUARTER)],

@@ -80,20 +80,23 @@ def tile_picked_treeup_relu_po_kernel(
         offs_sb = keep.tile([P, S // LIST_ROWS], U16, name="offs_sb")
         par_sb = keep.tile([P, S // LIST_ROWS], U16, name="par_sb")
         x_words_sb = keep.tile([P, T], I32, name="x_words_sb", align_bytes=64)
-        x_scales_sb = reused.tile([P, T], U8, name="x_scales_sb", align_bytes=64, offset=14336)
+        x_scales_sb = reused.tile([P, T], U8, name="x_scales_sb", align_bytes=64, offset=8192 + 1536)
         w1_raw = [
             reused.tile([P, PACK, K // 2], F32, name="w1_raw%d" % u, align_bytes=64, offset=4096 * u) for u in range(2)
         ]
-        w2_words_sb = reused.tile([P, K], I32, name="w2_words_sb", align_bytes=64, offset=0)
-        w2_scales_sb = reused.tile([P, K], U8, name="w2_scales_sb", align_bytes=64, offset=14336)
-        work = reused.tile([P, (PACK + 1) * HALF], F32, name="work", align_bytes=64, offset=4096)
+        w2_words_sb = reused.tile([P, K], I32, name="w2_words_sb", align_bytes=64, offset=8192)
+        w2_scales_sb = keep.tile([P, K], U8, name="w2_scales_sb", align_bytes=64)
+        w2_dealt_scales = keep.tile([P, K], U8, name="w2_dealt_scales", align_bytes=64)
+        work = reused.tile([P, (PACK + 1) * HALF], F32, name="work", align_bytes=64, offset=8192 + 3072)
         share_low = work[:, span(PACK - 1, 1, HALF)]
-        share_high = reused.tile([P, HALF], F32, name="share_high", align_bytes=64, offset=2048)
+        share_high = reused.tile([P, HALF], F32, name="share_high", align_bytes=64, offset=0)
         identity = keep.tile([P, P], F32, name="identity", align_bytes=64)
 
-        nc.gpsimd.memset(x_scales_sb[0:16, :].bitcast(I32), 0)
-        nc.vector.memset(x_scales_sb[32:64, :].bitcast(I32), 0)
-        nc.vector.memset(x_scales_sb[64:P, :].bitcast(I32), 0)
+        for rows in (x_scales_sb, w2_scales_sb):
+            nc.gpsimd.memset(rows[0:16, :].bitcast(I32), 0)
+            nc.vector.memset(rows[32:64, :].bitcast(I32), 0)
+            nc.vector.memset(rows[64:P, :].bitcast(I32), 0)
+        nc.vector.memset(w2_dealt_scales[:].bitcast(I32), 0)
         picked_scales = keep.tile([P, S], U8, name="picked_scales", align_bytes=64)
         nc.vector.memset(picked_scales[:].bitcast(I32), 0)
         make_identity(nc, identity[:])
@@ -101,40 +104,42 @@ def tile_picked_treeup_relu_po_kernel(
         w1_rows = w1.rearrange("(p j) c -> p j c", j=PACK)
         nc.sync.dma_start(offs_sb[:], offs)
         nc.sync.dma_start(out=x_scales_sb[16:32, :].bitcast(I32), in_=x_scales[0].bitcast(I32))
+        nc.sync.dma_start(out=x_words_sb[:], in_=x_words[0].rearrange("p c r -> p (c r)").bitcast(I32))
         nc.sync.dma_start(out=w1_raw[0][:], in_=w1_rows[:, :, : K // 2])
         nc.sync.dma_start(out=w1_raw[1][:], in_=w1_rows[:, :, K // 2 :])
-        nc.sync.dma_start(out=x_words_sb[:], in_=x_words[0].rearrange("p c r -> p (c r)").bitcast(I32))
+        nc.sync.dma_start(out=w2_scales_sb[16:32, :].bitcast(I32), in_=w2_scales[0].bitcast(I32))
         picked_rows = keep.tile([P, S], U8, name="picked_rows", align_bytes=64)
         nc.vector.tensor_copy(picked_rows[:], x_scales_sb[:].indirect(offs_sb[:]))
-        for q in range(QUADRANTS):
-            nc.sync.dma_start(
-                out=picked_scales[32 * q : 32 * q + 4, :].bitcast(I32),
-                in_=picked_rows[16 + 4 * q : 20 + 4 * q, :].bitcast(I32),
-            )
+        load_scale_rows(nc, picked_scales, picked_rows[16:32, :])
         nc.sync.dma_start(par_sb[:], par)
 
 
-        w1_bf = reused.tile([P, PACK, P, PACK], BF16, name="w1_bf", align_bytes=64, offset=16384)
+        w1_bf = keep.tile([P, PACK, P, PACK], BF16, name="w1_bf", align_bytes=64)
 
-        for u in range(2):
+        def round_w1(u, planes):
             nc.scalar.copy(
-                out=w1_bf[:, :, span(u, 1, P // 2), :].rearrange("p t m j -> p m j t"),
-                in_=w1_raw[u][:].rearrange("p j (m t) -> p m j t", t=PACK),
+                out=w1_bf[:, planes, span(u, 1, P // 2), :].rearrange("p t m j -> p m j t"),
+                in_=w1_raw[u][:].rearrange("p j (m t) -> p m j t", t=PACK)[:, :, :, planes],
             )
-        nc.sync.dma_start(out=w2_words_sb[:], in_=w2_words[0].rearrange("p c r -> p (c r)").bitcast(I32))
-        nc.vector.memset(w2_scales_sb[:].bitcast(I32), 0)
-        load_scale_rows(nc, w2_scales_sb, w2_scales[0])
-        nc.sync.dma_start(out=share_low, in_=share[:, :HALF])
-        nc.sync.dma_start(out=share_high[:], in_=share[:, HALF:])
+
         w1_codes = keep.tile([P, K], U32, name="w1_codes", align_bytes=64)
         w1_scales = keep.tile([P, K], U8, name="w1_scales", align_bytes=64)
-        quantise(nc, w1_codes, w1_scales, slice(0, K), w1_bf[:].rearrange("p t m j -> p (t m) j"))
-        picked_words = reused.tile([P, S], U32, name="picked_words", align_bytes=64, offset=16384)
-        for q in range(4):
-            nc.vector.tensor_copy(
-                picked_words[:, span(q, 1, QUARTER)],
-                x_words_sb[:].bitcast(U32).indirect(offs_sb[:, span(q, 1, QUARTER // LIST_ROWS)]),
-            )
+
+        def quantise_w1(first, count):
+            rounded = w1_bf[:, first : first + count, :, :].rearrange("p t m j -> p (t m) j")
+            quantise(nc, w1_codes, w1_scales, span(first, count, P), rounded)
+
+        picked_words = keep.tile([P, S], U32, name="picked_words", align_bytes=64)
+        nc.vector.tensor_copy(picked_words[:], x_words_sb[:].bitcast(U32).indirect(offs_sb[:]))
+        round_w1(0, slice(0, PACK))
+        round_w1(1, slice(0, 1))
+        quantise_w1(0, 1)
+        round_w1(1, slice(1, PACK))
+        quantise_w1(1, 1)
+        quantise_w1(2, 2)
+        nc.sync.dma_start(out=w2_words_sb[:], in_=w2_words[0].rearrange("p c r -> p (c r)").bitcast(I32))
+        nc.sync.dma_start(out=share_low, in_=share[:, :HALF])
+        nc.sync.dma_start(out=share_high[:], in_=share[:, HALF:])
 
         banks = [psum.tile([P, HALF], F32, name="bank%d" % c) for c in range(BANKS)]
         h = [keep.tile([P, S], F32, name="h%d" % t, align_bytes=64) for t in range(PACK)]
@@ -157,29 +162,25 @@ def tile_picked_treeup_relu_po_kernel(
         def relu(t, bank, first, count):
             nc.scalar.activation(out=h[t][:, span(first, count, BANK_COLS)], in_=place(bank, 0, count), func=ACT.Relu)
 
-        plane0 = ((0, 0, 2), (1, 2, 2), (2, 4, 2), (3, 6, 1), (4, 7, 1))
-        for bank, first, count in plane0:
-            first_product(0, place(bank, 0, count), span(first, count, BANK_COLS))
-            if (first + count) % 2 == 0:
-                q = (first + count) // 2 - 1
-                first_product(1, place(5 + q // 2, 2 * (q % 2), 2), span(q, 1, QUARTER))
-        for bank, first, count in plane0:
-            relu(0, bank, first, count)
-        for t in (1, 2, 3):
+        for q in range(4):
+            first_product(0, place(q, 0, 2), span(q, 1, QUARTER))
+            relu(0, q, 2 * q, 2)
+        for t, pair in ((1, (5, 6)), (2, (7, 4)), (3, (5, 6))):
             for u in range(2):
-                if t > 1:
-                    first_product(t, banks[5 + u][:], span(u, 1, HALF))
-                relu(t, 5 + u, 4 * u, 4)
+                first_product(t, banks[pair[u]][:], span(u, 1, HALF))
+                relu(t, pair[u], 4 * u, 4)
         for t in range(PACK):
             nc.sync.dma_start(out=own[:, t, :], in_=h[t][:, HALF:])
 
         w2_dealt_words = keep.tile([P, K], I32, name="w2_dealt_words", align_bytes=64)
-        w2_dealt_scales = keep.tile([P, K], U8, name="w2_dealt_scales", align_bytes=64)
-        for dealt, loaded in ((w2_dealt_words, w2_words_sb), (w2_dealt_scales, w2_scales_sb)):
+        w2_dealt_rows = keep.tile([P, K], U8, name="w2_dealt_rows", align_bytes=64)
+        for dealt, loaded in ((w2_dealt_rows, w2_scales_sb), (w2_dealt_words, w2_words_sb)):
             nc.vector.tensor_copy(
                 out=dealt[:].rearrange("p (t m) -> p t m", t=PACK),
                 in_=loaded[:].rearrange("p (m t) -> p t m", t=PACK),
             )
+
+        load_scale_rows(nc, w2_dealt_scales, w2_dealt_rows[16:32, :])
 
         z_turned = [keep.tile([P, K], BF16, name="z_turned%d" % c, align_bytes=64) for c in range(BANKS // 2)]
         z_stage = [keep.tile([P, 2 * K], BF16, name="z_stage%d" % u, align_bytes=64) for u in range(2)]

@@ -129,7 +129,7 @@ def tile_picked_treeup_relu_po_kernel(
             rounded = w1_bf[:, first : first + count, :, :].rearrange("p t m j -> p (t m) j")
             quantise(nc, w1_codes, w1_scales, span(first, count, P), rounded)
 
-        picked_words = keep.tile([P, S], U32, name="picked_words", align_bytes=64)
+        picked_words = reused.tile([P, S], U32, name="picked_words", align_bytes=64, offset=21504)
         nc.vector.tensor_copy(picked_words[:], x_words_sb[:].bitcast(U32).indirect(offs_sb[:]))
         round_w1(0, slice(0, PACK))
         round_w1(1, slice(0, 1))
@@ -182,7 +182,13 @@ def tile_picked_treeup_relu_po_kernel(
 
         load_scale_rows(nc, w2_dealt_scales, w2_dealt_rows[16:32, :])
 
-        z_turned = [keep.tile([P, K], BF16, name="z_turned%d" % c, align_bytes=64) for c in range(BANKS // 2)]
+        z_turned = {
+            (first, u): reused.tile(
+                [P, K], BF16, name="z_turned%d%d" % (first, u), align_bytes=64, offset=21504 + 512 * first + 2048 * u
+            )
+            for first in (0, 2)
+            for u in range(2)
+        }
         z_stage = [keep.tile([P, 2 * K], BF16, name="z_stage%d" % u, align_bytes=64) for u in range(2)]
         z_place = {0: (0, 0), 2: (1, 0), 4: (0, 0), 5: (1, 0), 6: (0, 1), 7: (1, 1)}
 
@@ -219,31 +225,40 @@ def tile_picked_treeup_relu_po_kernel(
             return banks[bank][:].rearrange("p (t j) -> p t j", t=PACK)
 
         taken_low = [work[:, span(slot, 1, HALF)] for slot in (0, 1, 2, 4)]
-        sum_bank = {0: 0, 1: 1, 2: 2, 3: 3}
+        sum_bank = {(0, 0): 0, (2, 0): 1, (0, 1): 2, (2, 1): 3}
         word_bank = {0: 7, 2: 4}
         y_bank = {0: 5, 1: 6, 2: 0, 3: 1, 4: 2, 5: 3, 6: 7, 7: 4}
 
-        def turn(t, c, values, start):
-            out = planes_in(sum_bank[c])[:, t, :]
+        def turn(t, c, values, is_h):
+            u, e = divmod(t, 2)
+            b = c % 2
+            out = banks[sum_bank[c - b, u]][:].rearrange("p (b e m) -> p b e m", b=2, e=2)[:, b, e, :]
             nc.tensor.matmul(
-                out, values[:, span(c, 1, BANK_COLS)], identity[:], start=start, stop=not start, is_transpose=True
+                out,
+                values[:, span(c, 1, BANK_COLS)],
+                identity[:],
+                start=is_h and (b, e) == (0, 0),
+                stop=not is_h and (b, e) == (1, 1),
+                is_transpose=True,
             )
 
-        def round_turned(c):
+        def words_in(first):
+            return banks[word_bank[first]][:].rearrange("p (b u j) -> p b u j", b=2, u=2)
+
+        def round_turned(first, u):
             nc.scalar.copy(
-                out=z_turned[c][:].rearrange("j (u m e) -> j u m e", u=2, e=2),
-                in_=banks[sum_bank[c]][:].rearrange("j (u e m) -> j u m e", u=2, e=2),
+                out=z_turned[first, u][:].rearrange("j (b m e) -> j b m e", b=2, e=2),
+                in_=banks[sum_bank[first, u]][:].rearrange("j (b e m) -> j b m e", b=2, e=2),
             )
 
-        def turn_back(first):
-            bank = banks[word_bank[first]][:].rearrange("p (b u j) -> p b u j", b=2, u=2)
-            for b in range(2):
-                pairs = z_turned[first + b][:].bitcast(F32)
-                for u in range(2):
-                    nc.tensor.transpose(bank[:, b, u, :], pairs[:, span(u, 1, P)], identity[:])
+        def copy_words(first):
+            for u in range(2):
+                pairs = z_turned[first, u][:].bitcast(F32)
+                for b in range(2):
+                    nc.tensor.transpose(words_in(first)[:, b, u, :], pairs[:, span(b, 1, P)], identity[:])
             nc.scalar.copy(
                 out=z_bf(first, 2).bitcast(F32).rearrange("p (b j u) -> p b j u", b=2, u=2),
-                in_=bank.rearrange("p b u j -> p b j u"),
+                in_=words_in(first).rearrange("p b u j -> p b j u"),
             )
 
         def quantise_z(first, count):
@@ -317,14 +332,14 @@ def tile_picked_treeup_relu_po_kernel(
             gather(taken_low[t][:, span(first, count, BANK_COLS)], t, first, count)
             for c in range(first, first + count):
                 turn(t, c, taken_low[t], False)
-                if t == PACK - 1:
-                    round_turned(c)
-            if t == PACK - 1 and (first + count) % 2 == 0:
-                turn_back(first + count - 2)
+                if t % 2 == 1 and c % 2 == 1:
+                    round_turned(c - 1, t // 2)
 
-        for t, groups in enumerate(((4,), (4,), (2, 2), (1, 1, 2))):
+        for t, groups in enumerate(((4,), (4,), (2, 2), (2, 2))):
             for first, count in runs(groups):
                 gather_low(t, first, count)
+        copy_words(0)
+        copy_words(2)
         gather_high(4, 2)
         quantise_z(0, 2)
         second_layer_by_pairs(0, 2, (5, 6))

@@ -20,11 +20,21 @@ T = 2048
 S = 1024
 LIST_ROWS = 16
 QUADRANTS = 4
-BANK_COLS = 128
-BANKS = S // BANK_COLS
+BANKS = 8
+GROUP = 128
+GROUPS = S // GROUP
+TURNED = GROUPS // 2
 HALF = S // 2
 QUARTER = S // 4
-STAGE_GROUPS = (2, 1, 1, 1, 1, 1, 1)
+SCALE_ROWS = slice(16, 32)
+STAGED_RUNS = (2, 1, 1, 1, 1, 1, 1)
+TURNED_RUNS = ((4,), (4,), (2, 2), (2, 2))
+
+W1_HALF_BYTES = PACK * (K // 2) * 4
+W2_WORDS_AT = 2 * W1_HALF_BYTES
+X_SCALES_AT = W2_WORDS_AT + 1536
+WORK_AT = W2_WORDS_AT + 3072
+SHARE_HIGH_AT = 0
 
 FLOPS = 2 * 2 * K * K * S
 
@@ -37,7 +47,7 @@ def span(first, count, width):
     return slice(first * width, (first + count) * width)
 
 
-def load_scale_rows(nc, tile, rows):
+def place_scale_rows(nc, tile, rows):
     for q in range(QUADRANTS):
         nc.sync.dma_start(out=tile[32 * q : 32 * q + 4, :].bitcast(I32), in_=rows[4 * q : 4 * q + 4, :].bitcast(I32))
 
@@ -48,9 +58,9 @@ def quantise(nc, codes, scales, cols, rounded):
     )
 
 
-def product(nc, bank, t, weight_codes, weight_scales, codes, scales, cols):
+def product(nc, out, t, weight_codes, weight_scales, codes, scales, cols):
     nc.tensor.matmul_mx(
-        out=bank[:, t, :],
+        out=out,
         lhsT=weight_codes[:, span(t, 1, P)].bitcast(FP8X4),
         lhsT_scale=weight_scales[:, span(t, 1, P)],
         rhs=codes[:, cols].bitcast(FP8X4),
@@ -80,16 +90,18 @@ def tile_picked_treeup_relu_po_kernel(
         offs_sb = keep.tile([P, S // LIST_ROWS], U16, name="offs_sb")
         par_sb = keep.tile([P, S // LIST_ROWS], U16, name="par_sb")
         x_words_sb = keep.tile([P, T], I32, name="x_words_sb", align_bytes=64)
-        x_scales_sb = reused.tile([P, T], U8, name="x_scales_sb", align_bytes=64, offset=8192 + 1536)
+        x_scales_sb = reused.tile([P, T], U8, name="x_scales_sb", align_bytes=64, offset=X_SCALES_AT)
         w1_raw = [
-            reused.tile([P, PACK, K // 2], F32, name="w1_raw%d" % u, align_bytes=64, offset=4096 * u) for u in range(2)
+            reused.tile([P, PACK, K // 2], F32, name="w1_raw%d" % u, align_bytes=64, offset=W1_HALF_BYTES * u)
+            for u in range(2)
         ]
-        w2_words_sb = reused.tile([P, K], I32, name="w2_words_sb", align_bytes=64, offset=8192)
+        w2_words_sb = reused.tile([P, K], I32, name="w2_words_sb", align_bytes=64, offset=W2_WORDS_AT)
         w2_scales_sb = keep.tile([P, K], U8, name="w2_scales_sb", align_bytes=64)
         w2_dealt_scales = keep.tile([P, K], U8, name="w2_dealt_scales", align_bytes=64)
-        work = reused.tile([P, (PACK + 1) * HALF], F32, name="work", align_bytes=64, offset=8192 + 3072)
-        share_low = work[:, span(PACK - 1, 1, HALF)]
-        share_high = reused.tile([P, HALF], F32, name="share_high", align_bytes=64, offset=0)
+        work = reused.tile([P, (PACK + 1) * HALF], F32, name="work", align_bytes=64, offset=WORK_AT)
+        share_slot = PACK - 1
+        share_low = work[:, span(share_slot, 1, HALF)]
+        share_high = reused.tile([P, HALF], F32, name="share_high", align_bytes=64, offset=SHARE_HIGH_AT)
         identity = keep.tile([P, P], F32, name="identity", align_bytes=64)
 
         for rows in (x_scales_sb, w2_scales_sb):
@@ -103,16 +115,15 @@ def tile_picked_treeup_relu_po_kernel(
 
         w1_rows = w1.rearrange("(p j) c -> p j c", j=PACK)
         nc.sync.dma_start(offs_sb[:], offs)
-        nc.sync.dma_start(out=x_scales_sb[16:32, :].bitcast(I32), in_=x_scales[0].bitcast(I32))
+        nc.sync.dma_start(out=x_scales_sb[SCALE_ROWS, :].bitcast(I32), in_=x_scales[0].bitcast(I32))
         nc.sync.dma_start(out=x_words_sb[:], in_=x_words[0].rearrange("p c r -> p (c r)").bitcast(I32))
         nc.sync.dma_start(out=w1_raw[0][:], in_=w1_rows[:, :, : K // 2])
         nc.sync.dma_start(out=w1_raw[1][:], in_=w1_rows[:, :, K // 2 :])
-        nc.sync.dma_start(out=w2_scales_sb[16:32, :].bitcast(I32), in_=w2_scales[0].bitcast(I32))
+        nc.sync.dma_start(out=w2_scales_sb[SCALE_ROWS, :].bitcast(I32), in_=w2_scales[0].bitcast(I32))
         picked_rows = keep.tile([P, S], U8, name="picked_rows", align_bytes=64)
         nc.vector.tensor_copy(picked_rows[:], x_scales_sb[:].indirect(offs_sb[:]))
-        load_scale_rows(nc, picked_scales, picked_rows[16:32, :])
+        place_scale_rows(nc, picked_scales, picked_rows[SCALE_ROWS, :])
         nc.sync.dma_start(par_sb[:], par)
-
 
         w1_bf = keep.tile([P, PACK, P, PACK], BF16, name="w1_bf", align_bytes=64)
 
@@ -129,7 +140,7 @@ def tile_picked_treeup_relu_po_kernel(
             rounded = w1_bf[:, first : first + count, :, :].rearrange("p t m j -> p (t m) j")
             quantise(nc, w1_codes, w1_scales, span(first, count, P), rounded)
 
-        picked_words = reused.tile([P, S], U32, name="picked_words", align_bytes=64, offset=21504)
+        picked_words = keep.tile([P, S], U32, name="picked_words", align_bytes=64)
         nc.vector.tensor_copy(picked_words[:], x_words_sb[:].bitcast(U32).indirect(offs_sb[:]))
         round_w1(0, slice(0, PACK))
         round_w1(1, slice(0, 1))
@@ -145,30 +156,16 @@ def tile_picked_treeup_relu_po_kernel(
         h = [keep.tile([P, S], F32, name="h%d" % t, align_bytes=64) for t in range(PACK)]
         own = keep.tile([P, PACK, HALF], F32, name="own", align_bytes=64)
 
-        def first_product(t, out, cols):
-            nc.tensor.matmul_mx(
-                out=out,
-                lhsT=w1_codes[:, span(t, 1, P)].bitcast(FP8X4),
-                lhsT_scale=w1_scales[:, span(t, 1, P)],
-                rhs=picked_words[:, cols].bitcast(FP8X4),
-                rhs_scale=picked_scales[:, cols],
-                start=True,
-                stop=True,
-            )
+        def first_layer(t, bank, cols):
+            out = banks[bank][:, : cols.stop - cols.start]
+            product(nc, out, t, w1_codes, w1_scales, picked_words, picked_scales, cols)
+            nc.scalar.activation(out=h[t][:, cols], in_=out, func=ACT.Relu)
 
-        def place(bank, slot, count):
-            return banks[bank][:, slot * BANK_COLS : (slot + count) * BANK_COLS]
-
-        def relu(t, bank, first, count):
-            nc.scalar.activation(out=h[t][:, span(first, count, BANK_COLS)], in_=place(bank, 0, count), func=ACT.Relu)
-
-        for q in range(4):
-            first_product(0, place(q, 0, 2), span(q, 1, QUARTER))
-            relu(0, q, 2 * q, 2)
+        for q in range(S // QUARTER):
+            first_layer(0, q, span(q, 1, QUARTER))
         for t, pair in ((1, (5, 6)), (2, (7, 4)), (3, (5, 6))):
             for u in range(2):
-                first_product(t, banks[pair[u]][:], span(u, 1, HALF))
-                relu(t, pair[u], 4 * u, 4)
+                first_layer(t, pair[u], span(u, 1, HALF))
         for t in range(PACK):
             nc.sync.dma_start(out=own[:, t, :], in_=h[t][:, HALF:])
 
@@ -179,55 +176,46 @@ def tile_picked_treeup_relu_po_kernel(
                 out=dealt[:].rearrange("p (t m) -> p t m", t=PACK),
                 in_=loaded[:].rearrange("p (m t) -> p t m", t=PACK),
             )
-
-        load_scale_rows(nc, w2_dealt_scales, w2_dealt_rows[16:32, :])
+        place_scale_rows(nc, w2_dealt_scales, w2_dealt_rows[SCALE_ROWS, :])
 
         z_turned = {
-            (first, u): reused.tile(
-                [P, K], BF16, name="z_turned%d%d" % (first, u), align_bytes=64, offset=21504 + 512 * first + 2048 * u
-            )
-            for first in (0, 2)
+            (first, u): keep.tile([P, K], BF16, name="z_turned%d%d" % (first, u), align_bytes=64)
+            for first in range(0, TURNED, 2)
             for u in range(2)
         }
         z_stage = [keep.tile([P, 2 * K], BF16, name="z_stage%d" % u, align_bytes=64) for u in range(2)]
-        z_place = {0: (0, 0), 2: (1, 0), 4: (0, 0), 5: (1, 0), 6: (0, 1), 7: (1, 1)}
-
-        def z_bf(first, count):
-            if first == BANKS - 1:
-                return y_bf[:, :K]
-            tile, slot = z_place[first]
-            return z_stage[tile][:, span(slot, count, K)]
-
         z_codes = keep.tile([P, S], U32, name="z_codes", align_bytes=64)
         z_scales = keep.tile([P, S], U8, name="z_scales", align_bytes=64)
         y_bf = keep.tile([P, S * PACK], BF16, name="y_bf", align_bytes=64)
         y_words = y_bf[:].rearrange("p (j t) -> p j t", t=PACK)
         y_codes = keep.tile([P, S], I32, name="y_codes", align_bytes=64)
         y_scales = keep.tile([P, S], U8, name="y_scales", align_bytes=64)
-        y = {}
-        for first, count in runs(STAGE_GROUPS):
-            staged = keep.tile([P, PACK, count * BANK_COLS], F32, name="y%d" % first, align_bytes=64)
-            for b in range(count):
-                y[first + b] = (staged, b)
+        z_bf = {
+            0: z_stage[0][:],
+            2: z_stage[1][:],
+            4: z_stage[0][:, :K],
+            5: z_stage[1][:, :K],
+            6: y_bf[:, span(2, 1, K)],
+            7: y_bf[:, :K],
+        }
+        staged = {
+            first: keep.tile([P, PACK, count * GROUP], F32, name="y%d" % first, align_bytes=64)
+            for first, count in runs(STAGED_RUNS)
+        }
         out_rows = out_0.rearrange("(p t) j -> p t j", t=PACK)
         out_words = out_1[0].rearrange("p c r -> p (c r)").bitcast(I32)
 
-        def gather(out, t, first, count):
-            shares = share_low if first < BANKS // 2 else share_high
-            nc.vector.tensor_tensor(
-                out,
-                h[t][:].indirect(par_sb[:, span(first, count, BANK_COLS // LIST_ROWS)]),
-                shares[:, span(first % (BANKS // 2), count, BANK_COLS)],
-                ALU.mult,
-            )
+        def followed(t, first, count):
+            return h[t][:].indirect(par_sb[:, span(first, count, GROUP // LIST_ROWS)])
 
-        def planes_in(bank):
-            return banks[bank][:].rearrange("p (t j) -> p t j", t=PACK)
+        def shares(first, count):
+            return (share_low if first < TURNED else share_high)[:, span(first % TURNED, count, GROUP)]
 
-        taken_low = [work[:, span(slot, 1, HALF)] for slot in (0, 1, 2, 4)]
-        sum_bank = {(0, 0): 0, (2, 0): 1, (0, 1): 2, (2, 1): 3}
+        taken_low = [work[:, span(slot, 1, HALF)] for slot in range(PACK + 1) if slot != share_slot]
+        sum_bank = {(first, u): first // 2 + 2 * u for first, u in z_turned}
         word_bank = {0: 7, 2: 4}
-        y_bank = {0: 5, 1: 6, 2: 0, 3: 1, 4: 2, 5: 3, 6: 7, 7: 4}
+        first_pair_banks = (5, 6)
+        y_bank = {2: 0, 3: 1, 4: 2, 5: 3, 6: word_bank[0], 7: word_bank[2]}
 
         def turn(t, c, values, is_h):
             u, e = divmod(t, 2)
@@ -235,15 +223,12 @@ def tile_picked_treeup_relu_po_kernel(
             out = banks[sum_bank[c - b, u]][:].rearrange("p (b e m) -> p b e m", b=2, e=2)[:, b, e, :]
             nc.tensor.matmul(
                 out,
-                values[:, span(c, 1, BANK_COLS)],
+                values[:, span(c, 1, GROUP)],
                 identity[:],
                 start=is_h and (b, e) == (0, 0),
                 stop=not is_h and (b, e) == (1, 1),
                 is_transpose=True,
             )
-
-        def words_in(first):
-            return banks[word_bank[first]][:].rearrange("p (b u j) -> p b u j", b=2, u=2)
 
         def round_turned(first, u):
             nc.scalar.copy(
@@ -251,103 +236,103 @@ def tile_picked_treeup_relu_po_kernel(
                 in_=banks[sum_bank[first, u]][:].rearrange("j (b e m) -> j b m e", b=2, e=2),
             )
 
-        def copy_words(first):
-            for u in range(2):
-                pairs = z_turned[first, u][:].bitcast(F32)
-                for b in range(2):
-                    nc.tensor.transpose(words_in(first)[:, b, u, :], pairs[:, span(b, 1, P)], identity[:])
-            nc.scalar.copy(
-                out=z_bf(first, 2).bitcast(F32).rearrange("p (b j u) -> p b j u", b=2, u=2),
-                in_=words_in(first).rearrange("p b u j -> p b j u"),
-            )
-
-        def quantise_z(first, count):
-            cols = span(first, count, BANK_COLS)
-            quantise(nc, z_codes, z_scales, cols, z_bf(first, count).rearrange("p (j t) -> p j t", t=PACK))
-
-        def taken_high(first, count):
-            start = (PACK if first == BANKS - 1 else PACK - 1) * HALF
-            return work[:, start : start + count * HALF].rearrange("p (t j) -> p t j", t=PACK)
-
-        def gather_high(first, count):
-            for t in range(PACK):
-                gather(taken_high(first, count)[:, t, :], t, first, count)
-
-        def add(c, taken):
-            nc.vector.tensor_tensor(
-                words_by_pairs(z_bf(c, 1).rearrange("p (j t) -> p j t", t=PACK)),
-                planes_by_pairs(own[:, :, span(c - BANKS // 2, 1, BANK_COLS)]),
-                planes_by_pairs(taken),
-                ALU.add,
-            )
-
-        def second_layer(c, scalar_rounds):
-            cols = span(c, 1, BANK_COLS)
-            bank = planes_in(y_bank[c])
-            for t in range(PACK):
-                product(nc, bank, t, w2_dealt_words, w2_dealt_scales, z_codes, z_scales, cols)
-            staged, b = y[c]
-            nc.scalar.copy(out=staged[:, :, span(b, 1, BANK_COLS)], in_=bank)
-            nc.sync.dma_start(out=out_rows[:, :, cols], in_=staged[:, :, span(b, 1, BANK_COLS)])
-            if scalar_rounds:
-                nc.scalar.copy(out=y_words[:, cols, :], in_=bank.rearrange("p t j -> p j t"))
-
-        def second_layer_by_pairs(first, count, pair_banks):
-            cols = span(first, count, BANK_COLS)
-            staged = y[first][0]
-            for pair in range(2):
-                bank = banks[pair_banks[pair]][:, : count * 2 * BANK_COLS].rearrange("p (t j) -> p t j", t=2)
-                for t in range(2):
-                    nc.tensor.matmul_mx(
-                        out=bank[:, t, :],
-                        lhsT=w2_dealt_words[:, span(2 * pair + t, 1, P)].bitcast(FP8X4),
-                        lhsT_scale=w2_dealt_scales[:, span(2 * pair + t, 1, P)],
-                        rhs=z_codes[:, cols].bitcast(FP8X4),
-                        rhs_scale=z_scales[:, cols],
-                        start=True,
-                        stop=True,
-                    )
-                planes = span(pair, 1, 2)
-                nc.scalar.copy(out=staged[:, planes, :], in_=bank)
-                nc.sync.dma_start(out=out_rows[:, planes, cols], in_=staged[:, planes, :])
-
-        def rounded_y(first, count):
-            start = (2 if first == 0 else first) * BANK_COLS
-            return y_words[:, start : start + count * BANK_COLS, :]
-
-        def vector_rounds(first, count):
-            nc.vector.tensor_copy(out=words_by_pairs(rounded_y(first, count)), in_=planes_by_pairs(y[first][0][:]))
-
-        def quantise_y(first, count):
-            done = slice(first * BANK_COLS, (first + count) * BANK_COLS)
-            quantise(nc, y_codes, y_scales, done, rounded_y(first, count))
-
-        def store_words(first, count):
-            done = span(first, count, BANK_COLS)
-            nc.sync.dma_start(out=out_words[:, done], in_=y_codes[:, done])
-
         def gather_low(t, first, count):
             for c in range(first, first + count):
                 turn(t, c, h[t], True)
-            gather(taken_low[t][:, span(first, count, BANK_COLS)], t, first, count)
+            nc.vector.tensor_tensor(
+                taken_low[t][:, span(first, count, GROUP)], followed(t, first, count), shares(first, count), ALU.mult
+            )
             for c in range(first, first + count):
                 turn(t, c, taken_low[t], False)
                 if t % 2 == 1 and c % 2 == 1:
                     round_turned(c - 1, t // 2)
 
-        for t, groups in enumerate(((4,), (4,), (2, 2), (2, 2))):
-            for first, count in runs(groups):
+        def turn_back(first):
+            bank = banks[word_bank[first]][:].rearrange("p (b u j) -> p b u j", b=2, u=2)
+            for u in range(2):
+                pairs = z_turned[first, u][:].bitcast(F32)
+                for b in range(2):
+                    nc.tensor.transpose(bank[:, b, u, :], pairs[:, span(b, 1, P)], identity[:])
+            nc.scalar.copy(
+                out=z_bf[first].bitcast(F32).rearrange("p (b j u) -> p b j u", b=2, u=2),
+                in_=bank.rearrange("p b u j -> p b j u"),
+            )
+
+        fetched_first = GROUPS - 2
+        fetched = taken_low[2][:, QUARTER:]
+
+        def taken_high(first, count):
+            start = (PACK if first == GROUPS - 1 else share_slot) * HALF
+            return work[:, start : start + count * HALF].rearrange("p (t j) -> p t j", t=PACK)
+
+        def gather_high(first, count):
+            for t in range(PACK):
+                if t == 0 and first >= fetched_first:
+                    values = fetched[:, span(first - fetched_first, count, GROUP)]
+                else:
+                    values = followed(t, first, count)
+                nc.vector.tensor_tensor(taken_high(first, count)[:, t, :], values, shares(first, count), ALU.mult)
+
+        def add(c, taken):
+            nc.vector.tensor_tensor(
+                words_by_pairs(z_bf[c].rearrange("p (j t) -> p j t", t=PACK)),
+                planes_by_pairs(own[:, :, span(c - TURNED, 1, GROUP)]),
+                planes_by_pairs(taken),
+                ALU.add,
+            )
+
+        def quantise_z(first, count):
+            cols = span(first, count, GROUP)
+            quantise(nc, z_codes, z_scales, cols, z_bf[first].rearrange("p (j t) -> p j t", t=PACK))
+
+        def second_layer(c, scalar_rounds):
+            cols = span(c, 1, GROUP)
+            bank = banks[y_bank[c]][:].rearrange("p (t j) -> p t j", t=PACK)
+            for t in range(PACK):
+                product(nc, bank[:, t, :], t, w2_dealt_words, w2_dealt_scales, z_codes, z_scales, cols)
+            nc.scalar.copy(out=staged[c][:], in_=bank)
+            nc.sync.dma_start(out=out_rows[:, :, cols], in_=staged[c][:])
+            if scalar_rounds:
+                nc.scalar.copy(out=y_words[:, cols, :], in_=bank.rearrange("p t j -> p j t"))
+
+        def second_layer_of_first_pair():
+            cols = span(0, 2, GROUP)
+            for pair in range(2):
+                bank = banks[first_pair_banks[pair]][:].rearrange("p (t j) -> p t j", t=2)
+                for t in range(2):
+                    product(nc, bank[:, t, :], 2 * pair + t, w2_dealt_words, w2_dealt_scales, z_codes, z_scales, cols)
+                planes = span(pair, 1, 2)
+                nc.scalar.copy(out=staged[0][:, planes, :], in_=bank)
+                nc.sync.dma_start(out=out_rows[:, planes, cols], in_=staged[0][:, planes, :])
+
+        def rounded_y(first, count):
+            return y_words[:, span(2 if first == 0 else first, count, GROUP), :]
+
+        def vector_rounds(first, count):
+            nc.vector.tensor_copy(out=words_by_pairs(rounded_y(first, count)), in_=planes_by_pairs(staged[first][:]))
+
+        def quantise_y(first, count):
+            quantise(nc, y_codes, y_scales, span(first, count, GROUP), rounded_y(first, count))
+
+        def store_words(first, count):
+            cols = span(first, count, GROUP)
+            nc.sync.dma_start(out=out_words[:, cols], in_=y_codes[:, cols])
+
+        for t, counts in enumerate(TURNED_RUNS):
+            for first, count in runs(counts):
                 gather_low(t, first, count)
-        copy_words(0)
-        copy_words(2)
+            if t == 2:
+                nc.scalar.activation(out=fetched, in_=followed(0, fetched_first, 2), func=ACT.Copy)
+        turn_back(0)
+        turn_back(2)
         gather_high(4, 2)
         quantise_z(0, 2)
-        second_layer_by_pairs(0, 2, (5, 6))
-        add(4, taken_high(4, 2)[:, :, :BANK_COLS])
+        second_layer_of_first_pair()
+        add(4, taken_high(4, 2)[:, :, :GROUP])
         quantise_z(2, 2)
-        second_layer(2, True)
+        second_layer(2, False)
         second_layer(3, True)
-        add(5, taken_high(4, 2)[:, :, BANK_COLS:])
+        add(5, taken_high(4, 2)[:, :, GROUP:])
         quantise_z(4, 1)
         second_layer(4, True)
         gather_high(6, 1)
@@ -358,6 +343,7 @@ def tile_picked_treeup_relu_po_kernel(
         quantise_z(6, 1)
         second_layer(6, True)
         add(7, taken_high(7, 1))
+        vector_rounds(2, 1)
         quantise_z(7, 1)
         second_layer(7, True)
         quantise_y(2, 4)

@@ -305,6 +305,32 @@ def tile_picked_treeup_relu_po_kernel(
                 nc.scalar.copy(out=staged[0][:, planes, :], in_=bank)
                 nc.sync.dma_start(out=out_rows[:, planes, cols], in_=staged[0][:, planes, :])
 
+        def last_halves():
+            c = GROUPS - 1
+            width = GROUP // 2
+            rounded = z_bf[c].rearrange("p (j t) -> p j t", t=PACK)
+            for u in range(2):
+                part = span(u, 1, width)
+                nc.vector.tensor_tensor(
+                    words_by_pairs(rounded[:, part, :]),
+                    planes_by_pairs(own[:, :, span(c - TURNED, 1, GROUP)][:, :, part]),
+                    planes_by_pairs(taken_high(c, 1)[:, :, part]),
+                    ALU.add,
+                )
+            for u, at in enumerate((y_bank[c], first_pair_banks[0])):
+                part = span(u, 1, width)
+                cols = span(2 * c + u, 1, width)
+                quantise(nc, z_codes, z_scales, cols, rounded[:, part, :])
+                bank = banks[at][:, : PACK * width].rearrange("p (t j) -> p t j", t=PACK)
+                for t in range(PACK):
+                    product(nc, bank[:, t, :], t, w2_dealt_words, w2_dealt_scales, z_codes, z_scales, cols)
+                nc.scalar.copy(out=staged[c][:, :, part], in_=bank)
+                if u == 0:
+                    vector_rounds(2, 1)
+                else:
+                    nc.sync.dma_start(out=out_rows[:, :, span(c, 1, GROUP)], in_=staged[c][:])
+                nc.scalar.copy(out=y_words[:, cols, :], in_=bank.rearrange("p t j -> p j t"))
+
         def rounded_y(first, count):
             return y_words[:, span(2 if first == 0 else first, count, GROUP), :]
 
@@ -342,18 +368,17 @@ def tile_picked_treeup_relu_po_kernel(
         gather_high(7, 1)
         quantise_z(6, 1)
         second_layer(6, True)
-        add(7, taken_high(7, 1))
-        vector_rounds(2, 1)
-        quantise_z(7, 1)
-        second_layer(7, True)
+        last_halves()
         quantise_y(2, 4)
         store_words(2, 4)
         vector_rounds(0, 2)
         quantise_y(6, 1)
         quantise_y(0, 2)
-        store_words(0, 2)
         quantise_y(7, 1)
-        store_words(6, 2)
+        ends = "p (a c) -> p a c"
+        nc.sync.dma_start(
+            out=out_words.rearrange(ends, c=QUARTER)[:, ::3, :], in_=y_codes[:].rearrange(ends, c=QUARTER)[:, ::3, :]
+        )
 
         for q in range(QUADRANTS):
             (nc.sync, nc.scalar)[q % 2].dma_start(

@@ -259,7 +259,7 @@ def tile_picked_treeup_relu_po_kernel(
             )
 
         fetched_first = GROUPS - 2
-        fetched = taken_low[2][:, QUARTER:]
+        fetched = (taken_low[2][:, QUARTER:], z_turned[2, 1][:].bitcast(F32))
 
         def taken_high(first, count):
             start = (PACK if first == GROUPS - 1 else share_slot) * HALF
@@ -267,8 +267,8 @@ def tile_picked_treeup_relu_po_kernel(
 
         def gather_high(first, count):
             for t in range(PACK):
-                if t == 0 and first >= fetched_first:
-                    values = fetched[:, span(first - fetched_first, count, GROUP)]
+                if t < len(fetched) and first >= fetched_first:
+                    values = fetched[t][:, span(first - fetched_first, count, GROUP)]
                 else:
                     values = followed(t, first, count)
                 nc.vector.tensor_tensor(taken_high(first, count)[:, t, :], values, shares(first, count), ALU.mult)
@@ -348,9 +348,10 @@ def tile_picked_treeup_relu_po_kernel(
             for first, count in runs(counts):
                 gather_low(t, first, count)
             if t == 2:
-                nc.scalar.activation(out=fetched, in_=followed(0, fetched_first, 2), func=ACT.Copy)
+                nc.scalar.activation(out=fetched[0], in_=followed(0, fetched_first, 2), func=ACT.Copy)
         turn_back(0)
         turn_back(2)
+        nc.scalar.activation(out=fetched[1], in_=followed(1, fetched_first, 2), func=ACT.Copy)
         gather_high(4, 2)
         quantise_z(0, 2)
         second_layer_of_first_pair()

@@ -89,19 +89,19 @@ def tile_picked_treeup_relu_po_kernel(
 
         offs_sb = keep.tile([P, S // LIST_ROWS], U16, name="offs_sb")
         par_sb = keep.tile([P, S // LIST_ROWS], U16, name="par_sb")
-        x_words_sb = keep.tile([P, T], I32, name="x_words_sb", align_bytes=64)
+        x_words_sb = keep.tile([P, T], I32, name="x_words_sb", align_bytes=256)
         x_scales_sb = reused.tile([P, T], U8, name="x_scales_sb", align_bytes=64, offset=X_SCALES_AT)
         w1_raw = [
-            reused.tile([P, PACK, K // 2], F32, name="w1_raw%d" % u, align_bytes=64, offset=W1_HALF_BYTES * u)
+            reused.tile([P, PACK, K // 2], F32, name="w1_raw%d" % u, align_bytes=256, offset=W1_HALF_BYTES * u)
             for u in range(2)
         ]
-        w2_words_sb = reused.tile([P, K], I32, name="w2_words_sb", align_bytes=64, offset=W2_WORDS_AT)
+        w2_words_sb = reused.tile([P, K], I32, name="w2_words_sb", align_bytes=256, offset=W2_WORDS_AT)
         w2_scales_sb = keep.tile([P, K], U8, name="w2_scales_sb", align_bytes=64)
         w2_dealt_scales = keep.tile([P, K], U8, name="w2_dealt_scales", align_bytes=64)
-        work = reused.tile([P, (PACK + 1) * HALF], F32, name="work", align_bytes=64, offset=WORK_AT)
+        work = reused.tile([P, (PACK + 1) * HALF], F32, name="work", align_bytes=256, offset=WORK_AT)
         share_slot = PACK - 1
         share_low = work[:, span(share_slot, 1, HALF)]
-        share_high = reused.tile([P, HALF], F32, name="share_high", align_bytes=64, offset=SHARE_HIGH_AT)
+        share_high = reused.tile([P, HALF], F32, name="share_high", align_bytes=256, offset=SHARE_HIGH_AT)
         identity = keep.tile([P, P], F32, name="identity", align_bytes=64)
 
         for rows in (x_scales_sb, w2_scales_sb):
@@ -153,8 +153,8 @@ def tile_picked_treeup_relu_po_kernel(
         nc.sync.dma_start(out=share_high[:], in_=share[:, HALF:])
 
         banks = [psum.tile([P, HALF], F32, name="bank%d" % c) for c in range(BANKS)]
-        h = [keep.tile([P, S], F32, name="h%d" % t, align_bytes=64) for t in range(PACK)]
-        own = keep.tile([P, PACK, HALF], F32, name="own", align_bytes=64)
+        h = [keep.tile([P, S], F32, name="h%d" % t, align_bytes=256) for t in range(PACK)]
+        own = keep.tile([P, PACK, HALF], F32, name="own", align_bytes=256)
 
         def first_layer(t, bank, cols):
             out = banks[bank][:, : cols.stop - cols.start]
@@ -188,7 +188,7 @@ def tile_picked_treeup_relu_po_kernel(
         z_scales = keep.tile([P, S], U8, name="z_scales", align_bytes=64)
         y_bf = keep.tile([P, S * PACK], BF16, name="y_bf", align_bytes=64)
         y_words = y_bf[:].rearrange("p (j t) -> p j t", t=PACK)
-        y_codes = keep.tile([P, S], I32, name="y_codes", align_bytes=64)
+        y_codes = keep.tile([P, S], I32, name="y_codes", align_bytes=256)
         y_scales = keep.tile([P, S], U8, name="y_scales", align_bytes=64)
         z_bf = {
             0: z_stage[0][:],
@@ -199,7 +199,7 @@ def tile_picked_treeup_relu_po_kernel(
             7: y_bf[:, :K],
         }
         staged = {
-            first: keep.tile([P, PACK, count * GROUP], F32, name="y%d" % first, align_bytes=64)
+            first: keep.tile([P, PACK, count * GROUP], F32, name="y%d" % first, align_bytes=256)
             for first, count in runs(STAGED_RUNS)
         }
         out_rows = out_0.rearrange("(p t) j -> p t j", t=PACK)

from contextlib import ExitStack

import concourse.mybir as mybir
from concourse.masks import make_identity

F32 = mybir.dt.float32
BF16 = mybir.dt.bfloat16
I32 = mybir.dt.int32
U32 = mybir.dt.uint32
U16 = mybir.dt.uint16
U8 = mybir.dt.uint8
FP8X4 = mybir.dt.float8_e4m3fn_x4
ALU = mybir.AluOpType
ACT = mybir.ActivationFunctionType

P = 128
PACK = 4
K = 512
T = 2048
S = 1024
LIST_ROWS = 16
QUADRANTS = 4
BANKS = 8
GROUP = 128
GROUPS = S // GROUP
TURNED = GROUPS // 2
HALF = S // 2
QUARTER = S // 4
SCALE_ROWS = slice(16, 32)
STAGED_RUNS = (2, 1, 1, 1, 1, 1, 1)
TURNED_RUNS = ((4,), (4,), (2, 2), (2, 2))

W1_HALF_BYTES = PACK * (K // 2) * 4
W2_WORDS_AT = 2 * W1_HALF_BYTES
X_SCALES_AT = W2_WORDS_AT + 1536
WORK_AT = W2_WORDS_AT + 3072
SHARE_HIGH_AT = 0

FLOPS = 2 * 2 * K * K * S


def runs(counts):
    return [(sum(counts[:g]), count) for g, count in enumerate(counts)]


def span(first, count, width):
    return slice(first * width, (first + count) * width)


def place_scale_rows(nc, tile, rows):
    for q in range(QUADRANTS):
        nc.sync.dma_start(out=tile[32 * q : 32 * q + 4, :].bitcast(I32), in_=rows[4 * q : 4 * q + 4, :].bitcast(I32))


def quantise(nc, codes, scales, cols, rounded):
    nc.vector.quantize_mx(
        out=codes[:, cols].bitcast(FP8X4), scales=scales[:, cols], in_=rounded.rearrange("p j t -> p (j t)")
    )


def product(nc, out, t, weight_codes, weight_scales, codes, scales, cols):
    nc.tensor.matmul_mx(
        out=out,
        lhsT=weight_codes[:, span(t, 1, P)].bitcast(FP8X4),
        lhsT_scale=weight_scales[:, span(t, 1, P)],
        rhs=codes[:, cols].bitcast(FP8X4),
        rhs_scale=scales[:, cols],
        start=True,
        stop=True,
    )


def planes_by_pairs(planes):
    return planes.rearrange("p t (a i) -> p a t i", i=2)


def words_by_pairs(rounded):
    return rounded.rearrange("p (a i) t -> p a t i", i=2)


def tile_picked_treeup_relu_po_kernel(
    tc, x_words, x_scales, w1, w2_words, w2_scales, share, offs, par, out_0, out_1, out_2
):
    nc = tc.nc
    with ExitStack() as ctx:
        keep = ctx.enter_context(tc.tile_pool(name="keep", bufs=1))
        reused = ctx.enter_context(tc.tile_pool(name="reused", bufs=1))
        psum = ctx.enter_context(tc.psum_pool(name="psum", bufs=1))

        offs_sb = keep.tile([P, S // LIST_ROWS], U16, name="offs_sb")
        par_sb = keep.tile([P, S // LIST_ROWS], U16, name="par_sb")
        x_words_sb = keep.tile([P, T], I32, name="x_words_sb", align_bytes=256)
        x_scales_sb = reused.tile([P, T], U8, name="x_scales_sb", align_bytes=64, offset=X_SCALES_AT)
        w1_raw = [
            reused.tile([P, PACK, K // 2], F32, name="w1_raw%d" % u, align_bytes=256, offset=W1_HALF_BYTES * u)
            for u in range(2)
        ]
        w2_words_sb = reused.tile([P, K], I32, name="w2_words_sb", align_bytes=256, offset=W2_WORDS_AT)
        w2_scales_sb = keep.tile([P, K], U8, name="w2_scales_sb", align_bytes=64)
        w2_dealt_scales = keep.tile([P, K], U8, name="w2_dealt_scales", align_bytes=64)
        work = reused.tile([P, (PACK + 1) * HALF], F32, name="work", align_bytes=256, offset=WORK_AT)
        share_slot = PACK - 1
        share_low = work[:, span(share_slot, 1, HALF)]
        share_high = reused.tile([P, HALF], F32, name="share_high", align_bytes=256, offset=SHARE_HIGH_AT)
        identity = keep.tile([P, P], F32, name="identity", align_bytes=64)

        for rows in (x_scales_sb, w2_scales_sb):
            nc.gpsimd.memset(rows[0:16, :].bitcast(I32), 0)
            nc.vector.memset(rows[32:64, :].bitcast(I32), 0)
            nc.vector.memset(rows[64:P, :].bitcast(I32), 0)
        nc.vector.memset(w2_dealt_scales[:].bitcast(I32), 0)
        picked_scales = keep.tile([P, S], U8, name="picked_scales", align_bytes=64)
        nc.vector.memset(picked_scales[:].bitcast(I32), 0)
        make_identity(nc, identity[:])

        w1_rows = w1.rearrange("(p j) c -> p j c", j=PACK)
        nc.sync.dma_start(offs_sb[:], offs)
        nc.sync.dma_start(out=x_scales_sb[SCALE_ROWS, :].bitcast(I32), in_=x_scales[0].bitcast(I32))
        nc.sync.dma_start(out=x_words_sb[:], in_=x_words[0].rearrange("p c r -> p (c r)").bitcast(I32))
        nc.sync.dma_start(out=w1_raw[0][:], in_=w1_rows[:, :, : K // 2])
        nc.sync.dma_start(out=w1_raw[1][:], in_=w1_rows[:, :, K // 2 :])
        nc.sync.dma_start(out=w2_scales_sb[SCALE_ROWS, :].bitcast(I32), in_=w2_scales[0].bitcast(I32))
        picked_rows = keep.tile([P, S], U8, name="picked_rows", align_bytes=64)
        nc.vector.tensor_copy(picked_rows[:], x_scales_sb[:].indirect(offs_sb[:]))
        place_scale_rows(nc, picked_scales, picked_rows[SCALE_ROWS, :])
        nc.sync.dma_start(par_sb[:], par)

        w1_bf = keep.tile([P, PACK, P, PACK], BF16, name="w1_bf", align_bytes=64)

        def round_w1(u, planes):
            nc.scalar.copy(
                out=w1_bf[:, planes, span(u, 1, P // 2), :].rearrange("p t m j -> p m j t"),
                in_=w1_raw[u][:].rearrange("p j (m t) -> p m j t", t=PACK)[:, :, :, planes],
            )

        w1_codes = keep.tile([P, K], U32, name="w1_codes", align_bytes=64)
        w1_scales = keep.tile([P, K], U8, name="w1_scales", align_bytes=64)

        def quantise_w1(first, count):
            rounded = w1_bf[:, first : first + count, :, :].rearrange("p t m j -> p (t m) j")
            quantise(nc, w1_codes, w1_scales, span(first, count, P), rounded)

        picked_words = keep.tile([P, S], U32, name="picked_words", align_bytes=64)
        nc.vector.tensor_copy(picked_words[:], x_words_sb[:].bitcast(U32).indirect(offs_sb[:]))
        round_w1(0, slice(0, PACK))
        round_w1(1, slice(0, 1))
        quantise_w1(0, 1)
        round_w1(1, slice(1, PACK))
        quantise_w1(1, 1)
        quantise_w1(2, 2)
        nc.sync.dma_start(out=w2_words_sb[:], in_=w2_words[0].rearrange("p c r -> p (c r)").bitcast(I32))
        nc.sync.dma_start(out=share_low, in_=share[:, :HALF])
        nc.sync.dma_start(out=share_high[:], in_=share[:, HALF:])

        banks = [psum.tile([P, HALF], F32, name="bank%d" % c) for c in range(BANKS)]
        h = [keep.tile([P, S], F32, name="h%d" % t, align_bytes=256) for t in range(PACK)]
        own = keep.tile([P, PACK, HALF], F32, name="own", align_bytes=256)

        def first_layer(t, bank, cols):
            out = banks[bank][:, : cols.stop - cols.start]
            product(nc, out, t, w1_codes, w1_scales, picked_words, picked_scales, cols)
            nc.scalar.activation(out=h[t][:, cols], in_=out, func=ACT.Relu)

        for q in range(S // QUARTER):
            first_layer(0, q, span(q, 1, QUARTER))
        for t, pair in ((1, (5, 6)), (2, (7, 4)), (3, (5, 6))):
            for u in range(2):
                first_layer(t, pair[u], span(u, 1, HALF))
        for t in range(PACK):
            nc.sync.dma_start(out=own[:, t, :], in_=h[t][:, HALF:])

        w2_dealt_words = keep.tile([P, K], I32, name="w2_dealt_words", align_bytes=64)
        w2_dealt_rows = keep.tile([P, K], U8, name="w2_dealt_rows", align_bytes=64)
        for dealt, loaded in ((w2_dealt_rows, w2_scales_sb), (w2_dealt_words, w2_words_sb)):
            nc.vector.tensor_copy(
                out=dealt[:].rearrange("p (t m) -> p t m", t=PACK),
                in_=loaded[:].rearrange("p (m t) -> p t m", t=PACK),
            )
        place_scale_rows(nc, w2_dealt_scales, w2_dealt_rows[SCALE_ROWS, :])

        z_turned = {
            (first, u): keep.tile([P, K], BF16, name="z_turned%d%d" % (first, u), align_bytes=64)
            for first in range(0, TURNED, 2)
            for u in range(2)
        }
        z_stage = [keep.tile([P, 2 * K], BF16, name="z_stage%d" % u, align_bytes=64) for u in range(2)]
        z_codes = keep.tile([P, S], U32, name="z_codes", align_bytes=64)
        z_scales = keep.tile([P, S], U8, name="z_scales", align_bytes=64)
        y_bf = keep.tile([P, S * PACK], BF16, name="y_bf", align_bytes=64)
        y_words = y_bf[:].rearrange("p (j t) -> p j t", t=PACK)
        y_codes = keep.tile([P, S], I32, name="y_codes", align_bytes=256)
        y_scales = keep.tile([P, S], U8, name="y_scales", align_bytes=64)
        z_bf = {
            0: z_stage[0][:],
            2: z_stage[1][:],
            4: z_stage[0][:, :K],
            5: z_stage[1][:, :K],
            6: y_bf[:, span(2, 1, K)],
            7: y_bf[:, :K],
        }
        staged = {
            first: keep.tile([P, PACK, count * GROUP], F32, name="y%d" % first, align_bytes=256)
            for first, count in runs(STAGED_RUNS)
        }
        out_rows = out_0.rearrange("(p t) j -> p t j", t=PACK)
        out_words = out_1[0].rearrange("p c r -> p (c r)").bitcast(I32)

        def followed(t, first, count):
            return h[t][:].indirect(par_sb[:, span(first, count, GROUP // LIST_ROWS)])

        def shares(first, count):
            return (share_low if first < TURNED else share_high)[:, span(first % TURNED, count, GROUP)]

        taken_low = [work[:, span(slot, 1, HALF)] for slot in range(PACK + 1) if slot != share_slot]
        sum_bank = {(first, u): first // 2 + 2 * u for first, u in z_turned}
        word_bank = {0: 7, 2: 4}
        first_pair_banks = (5, 6)
        y_bank = {2: 0, 3: 1, 4: 2, 5: 3, 6: word_bank[0], 7: word_bank[2]}

        def turn(t, c, values, is_h):
            u, e = divmod(t, 2)
            b = c % 2
            out = banks[sum_bank[c - b, u]][:].rearrange("p (b e m) -> p b e m", b=2, e=2)[:, b, e, :]
            nc.tensor.matmul(
                out,
                values[:, span(c, 1, GROUP)],
                identity[:],
                start=is_h and (b, e) == (0, 0),
                stop=not is_h and (b, e) == (1, 1),
                is_transpose=True,
            )

        def round_turned(first, u):
            nc.scalar.copy(
                out=z_turned[first, u][:].rearrange("j (b m e) -> j b m e", b=2, e=2),
                in_=banks[sum_bank[first, u]][:].rearrange("j (b e m) -> j b m e", b=2, e=2),
            )

        def gather_low(t, first, count):
            for c in range(first, first + count):
                turn(t, c, h[t], True)
            nc.vector.tensor_tensor(
                taken_low[t][:, span(first, count, GROUP)], followed(t, first, count), shares(first, count), ALU.mult
            )
            for c in range(first, first + count):
                turn(t, c, taken_low[t], False)
                if t % 2 == 1 and c % 2 == 1:
                    round_turned(c - 1, t // 2)

        def turn_back(first):
            bank = banks[word_bank[first]][:].rearrange("p (b u j) -> p b u j", b=2, u=2)
            for u in range(2):
                pairs = z_turned[first, u][:].bitcast(F32)
                for b in range(2):
                    nc.tensor.transpose(bank[:, b, u, :], pairs[:, span(b, 1, P)], identity[:])
            nc.scalar.copy(
                out=z_bf[first].bitcast(F32).rearrange("p (b j u) -> p b j u", b=2, u=2),
                in_=bank.rearrange("p b u j -> p b j u"),
            )

        fetched_first = GROUPS - 2
        fetched = (taken_low[2][:, QUARTER:], z_turned[2, 1][:].bitcast(F32))

        def taken_high(first, count):
            start = (PACK if first == GROUPS - 1 else share_slot) * HALF
            return work[:, start : start + count * HALF].rearrange("p (t j) -> p t j", t=PACK)

        def gather_high(first, count):
            for t in range(PACK):
                if t < len(fetched) and first >= fetched_first:
                    values = fetched[t][:, span(first - fetched_first, count, GROUP)]
                else:
                    values = followed(t, first, count)
                nc.vector.tensor_tensor(taken_high(first, count)[:, t, :], values, shares(first, count), ALU.mult)

        def add(c, taken):
            nc.vector.tensor_tensor(
                words_by_pairs(z_bf[c].rearrange("p (j t) -> p j t", t=PACK)),
                planes_by_pairs(own[:, :, span(c - TURNED, 1, GROUP)]),
                planes_by_pairs(taken),
                ALU.add,
            )

        def quantise_z(first, count):
            cols = span(first, count, GROUP)
            quantise(nc, z_codes, z_scales, cols, z_bf[first].rearrange("p (j t) -> p j t", t=PACK))

        def second_layer(c, scalar_rounds):
            cols = span(c, 1, GROUP)
            bank = banks[y_bank[c]][:].rearrange("p (t j) -> p t j", t=PACK)
            for t in range(PACK):
                product(nc, bank[:, t, :], t, w2_dealt_words, w2_dealt_scales, z_codes, z_scales, cols)
            nc.scalar.copy(out=staged[c][:], in_=bank)
            nc.sync.dma_start(out=out_rows[:, :, cols], in_=staged[c][:])
            if scalar_rounds:
                nc.scalar.copy(out=y_words[:, cols, :], in_=bank.rearrange("p t j -> p j t"))

        def second_layer_of_first_pair():
            cols = span(0, 2, GROUP)
            for pair in range(2):
                bank = banks[first_pair_banks[pair]][:].rearrange("p (t j) -> p t j", t=2)
                for t in range(2):
                    product(nc, bank[:, t, :], 2 * pair + t, w2_dealt_words, w2_dealt_scales, z_codes, z_scales, cols)
                planes = span(pair, 1, 2)
                nc.scalar.copy(out=staged[0][:, planes, :], in_=bank)
                nc.sync.dma_start(out=out_rows[:, planes, cols], in_=staged[0][:, planes, :])

        def last_halves():
            c = GROUPS - 1
            width = GROUP // 2
            rounded = z_bf[c].rearrange("p (j t) -> p j t", t=PACK)
            for u in range(2):
                part = span(u, 1, width)
                nc.vector.tensor_tensor(
                    words_by_pairs(rounded[:, part, :]),
                    planes_by_pairs(own[:, :, span(c - TURNED, 1, GROUP)][:, :, part]),
                    planes_by_pairs(taken_high(c, 1)[:, :, part]),
                    ALU.add,
                )
            for u, at in enumerate((y_bank[c], first_pair_banks[0])):
                part = span(u, 1, width)
                cols = span(2 * c + u, 1, width)
                quantise(nc, z_codes, z_scales, cols, rounded[:, part, :])
                bank = banks[at][:, : PACK * width].rearrange("p (t j) -> p t j", t=PACK)
                for t in range(PACK):
                    product(nc, bank[:, t, :], t, w2_dealt_words, w2_dealt_scales, z_codes, z_scales, cols)
                nc.scalar.copy(out=staged[c][:, :, part], in_=bank)
                if u == 0:
                    vector_rounds(2, 1)
                else:
                    nc.sync.dma_start(out=out_rows[:, :, span(c, 1, GROUP)], in_=staged[c][:])
                nc.scalar.copy(out=y_words[:, cols, :], in_=bank.rearrange("p t j -> p j t"))

        def rounded_y(first, count):
            return y_words[:, span(2 if first == 0 else first, count, GROUP), :]

        def vector_rounds(first, count):
            nc.vector.tensor_copy(out=words_by_pairs(rounded_y(first, count)), in_=planes_by_pairs(staged[first][:]))

        def quantise_y(first, count):
            quantise(nc, y_codes, y_scales, span(first, count, GROUP), rounded_y(first, count))

        def store_words(first, count):
            cols = span(first, count, GROUP)
            nc.sync.dma_start(out=out_words[:, cols], in_=y_codes[:, cols])

        for t, counts in enumerate(TURNED_RUNS):
            for first, count in runs(counts):
                gather_low(t, first, count)
            if t == 2:
                nc.scalar.activation(out=fetched[0], in_=followed(0, fetched_first, 2), func=ACT.Copy)
        turn_back(0)
        turn_back(2)
        nc.scalar.activation(out=fetched[1], in_=followed(1, fetched_first, 2), func=ACT.Copy)
        gather_high(4, 2)
        quantise_z(0, 2)
        second_layer_of_first_pair()
        add(4, taken_high(4, 2)[:, :, :GROUP])
        quantise_z(2, 2)
        second_layer(2, False)
        second_layer(3, True)
        add(5, taken_high(4, 2)[:, :, GROUP:])
        quantise_z(4, 1)
        second_layer(4, True)
        gather_high(6, 1)
        quantise_z(5, 1)
        second_layer(5, True)
        add(6, taken_high(6, 1))
        gather_high(7, 1)
        quantise_z(6, 1)
        second_layer(6, True)
        last_halves()
        quantise_y(2, 4)
        store_words(2, 4)
        vector_rounds(0, 2)
        quantise_y(6, 1)
        quantise_y(0, 2)
        quantise_y(7, 1)
        ends = "p (a c) -> p a c"
        nc.sync.dma_start(
            out=out_words.rearrange(ends, c=QUARTER)[:, ::3, :], in_=y_codes[:].rearrange(ends, c=QUARTER)[:, ::3, :]
        )

        for q in range(QUADRANTS):
            (nc.sync, nc.scalar)[q % 2].dma_start(
                out=out_2[0][4 * q : 4 * q + 4, :].bitcast(I32), in_=y_scales[32 * q : 32 * q + 4, :].bitcast(I32)
            )
